import numpy as np
import ml_dtypes


def mxq(x, axis, fmt="e4m3"):
    dtype, down = {"e4m3": (ml_dtypes.float8_e4m3fn, 7), "e5m2": (ml_dtypes.float8_e5m2, 14)}[fmt]
    v = np.moveaxis(np.asarray(x, np.float32).astype(ml_dtypes.bfloat16).astype(np.float64), axis, -1)
    blocks = v.reshape(v.shape[:-1] + (-1, 32))
    amax = np.abs(blocks).max(-1, keepdims=True)
    byte = np.maximum(np.where(amax > 0, np.frexp(amax)[1] - 1 + 127, 0) - down, 1)
    scale = np.exp2(byte - 127.0)
    codes = (blocks / scale).astype(np.float32).astype(dtype).astype(np.float64)
    return np.moveaxis((codes * scale).reshape(v.shape), -1, axis)


WIDE = False


def mx_kscale(k):
    if not WIDE:
        return np.ones(k)
    levels = np.array([10, -10, 5, -5, 0])
    if k % 512:
        return np.exp2(np.random.permutation(np.resize(levels, k // 32))).repeat(32)
    a = np.empty((k // 512, 16))
    for p in range(k // 512):
        a[p, :8] = np.random.permutation(np.resize(levels, 8))
        for g in range(8):
            far = levels[np.abs(levels - a[p, g]) >= 10]
            a[p, g + 8] = far[np.random.randint(len(far))]
    return np.exp2(a.ravel()).repeat(32)


def f64(x):
    return np.asarray(x).astype(np.float64)


def striped(idx):
    return np.tile(idx.reshape(-1, 16).T, (8, 1)).astype(np.uint16)


def unstriped(offs):
    return offs[:16].T.reshape(-1).astype(np.int64)


E2M1 = np.array([0.0, 0.5, 1.0, 1.5, 2.0, 3.0, 4.0, 6.0, -0.0, -0.5, -1.0, -1.5, -2.0, -3.0, -4.0, -6.0])


def pack_weight(w, fmt):
    k, n = w.shape
    w = f64(np.asarray(w, np.float32).astype(ml_dtypes.bfloat16)).reshape(k // 32, 32, n)
    amax = np.abs(w).max(1)
    if fmt == "e4m3":
        byte = np.frexp(amax)[1] - 1 + 127 - 7
    else:
        mant, ex = np.frexp(amax / 6.0)
        byte = np.where(mant > 0.5, ex, ex - 1) + 127
    byte = np.clip(np.where(amax > 0, byte, 1), 1, 254)
    scaled = (w * np.exp2(127.0 - byte)[:, None, :]).reshape(k, n).astype(np.float32)
    by_word = np.ascontiguousarray(scaled.reshape(k // 512, 128, 4, n).transpose(0, 1, 3, 2))
    if fmt == "e4m3":
        words = by_word.astype(ml_dtypes.float8_e4m3fn).view(np.uint8)
    else:
        c = by_word.astype(ml_dtypes.float4_e2m1fn).view(np.uint8) & 0xF
        words = (c[..., 0::2] | (c[..., 1::2] << 4)).reshape(k // 512, 128, 2 * n)
    return np.ascontiguousarray(words), np.ascontiguousarray(byte.astype(np.uint8).reshape(k // 512, 16, n))


def unpack_weight(words, scales, fmt):
    g, _, n = scales.shape
    words = np.ascontiguousarray(words).reshape(g, 128, n, -1)
    if fmt == "e4m3":
        vals = words.view(ml_dtypes.float8_e4m3fn).astype(np.float64)
    else:
        nib = np.empty((g, 128, n, 4), np.uint8)
        nib[..., 0::2] = words & 0xF
        nib[..., 1::2] = words >> 4
        vals = E2M1[nib]
    vals = vals * np.repeat(np.exp2(scales.astype(np.float64) - 127.0), 8, axis=1)[..., None]
    return vals.transpose(0, 1, 3, 2).reshape(g * 512, n)


def silu(v):
    return v / (1.0 + np.exp(-np.maximum(v, -700.0)))


K, T, Q, E, C, D, H = 512, 768, 512, 6, 256, 256, 512
N = 256


def by_expert(wq, xq, C):
    return np.concatenate([wq[e].T @ xq[:, e * C:(e + 1) * C] for e in range(E)], axis=1)


def setup_inputs():
    n = np.random.standard_normal
    s = mx_kscale(K)
    u = mx_kscale(H)
    first = np.random.permutation(np.repeat(np.arange(E), T // E))
    second = (first + 1 + np.random.permutation(np.repeat(np.arange(E - 1), -(-T // (E - 1)))[:T])) % E
    while np.bincount(second, minlength=E).max() != T // E:
        load = np.bincount(second, minlength=E); hi, lo = int(load.argmax()), int(load.argmin())
        t = np.flatnonzero((second == hi) & (first != lo))[0]; second[t] = lo
    slot_token = np.empty(E * C, np.int64); pos = np.empty((2, T), np.int64); fill = np.zeros(E, np.int64)
    place = np.stack([np.random.permutation(C) for _ in range(E)])
    for r, deal in enumerate((first, second)):
        for t in np.random.permutation(T):
            e = deal[t]; j = e * C + place[e, fill[e]]; fill[e] += 1; slot_token[j] = t; pos[r, t] = j
    g = np.random.uniform(0.2, 0.8, T)
    slots2 = np.concatenate([np.random.permutation(Q)[:D] for e in range(E)])
    x = pack_weight(n((K, Q)) * s[:, None], "e4m3")
    w1 = [pack_weight(m, "e2m1") for m in n((E, K, H)) / np.sqrt(K) / s[None, :, None] * u]
    w2 = [pack_weight(m, "e2m1") for m in n((E, H, N)) / np.sqrt(H) / u[None, :, None]]
    return {
        "x_words": x[0],
        "x_scales": x[1],
        "xo": (n((K, T)) * s[:, None]).astype(np.float32),
        "w1_words": np.stack([m[0] for m in w1]),
        "w1_scales": np.stack([m[1] for m in w1]),
        "w2_words": np.stack([m[0] for m in w2]),
        "w2_scales": np.stack([m[1] for m in w2]),
        "gate": np.stack([np.tile(g, (128, 1)), np.tile(1.0 - g, (128, 1))]).astype(np.float32),
        "offs": striped(slot_token),
        "pos1": striped(pos[0]),
        "pos2": striped(pos[1]),
        "offs2": striped(slots2),
    }


def reference(x_words, x_scales, xo, w1_words, w1_scales, w2_words, w2_scales, gate, offs, pos1, pos2, offs2):
    w1 = np.stack([unpack_weight(w1_words[e], w1_scales[e], "e2m1") for e in range(E)])
    w2 = np.stack([unpack_weight(w2_words[e], w2_scales[e], "e2m1") for e in range(E)])
    idx, idx2 = unstriped(offs), unstriped(offs2)
    xq = mxq(f64(xo)[:, idx], 0, "e4m3")
    rq = unpack_weight(x_words, x_scales, "e4m3")[:, idx2]
    h = silu(by_expert(w1, xq, C))
    y = by_expert(w2, mxq(h, 0, "e4m3"), C)
    h = silu(by_expert(w1, rq, D))
    z = by_expert(w2, mxq(h, 0, "e4m3"), D)
    own = sum(f64(gate[r, :1]) * y[:, unstriped(p)] for r, p in enumerate((pos1, pos2)))
    return np.concatenate([own, z], axis=1)

@@ -1,0 +1,266 @@
+from contextlib import ExitStack
+
+import concourse.mybir as mybir
+
+K, T, Q, E, C, H, N = 512, 768, 512, 6, 256, 512, 256
+S = E * C
+FLOPS = 2 * 2 * S * (K * H + H * N)
+
+F32 = mybir.dt.float32
+BF16 = mybir.dt.bfloat16
+I32 = mybir.dt.int32
+U32 = mybir.dt.uint32
+U16 = mybir.dt.uint16
+U8 = mybir.dt.uint8
+FP8X4 = mybir.dt.float8_e4m3fn_x4
+FP4X4 = mybir.dt.float4_e2m1fn_x4
+SILU = mybir.ActivationFunctionType.Silu
+MULT = mybir.AluOpType.mult
+ADD = mybir.AluOpType.add
+
+P = 128
+LIST_COLS = C // 16
+ZAFTER = ("rs1", "", "rs2", "", "", "")
+
+
+def tile_moe_loc_mlp_silu_kernel(
+    tc, x_words, x_scales, xo, w1_words, w1_scales, w2_words, w2_scales, gate, offs, pos1, pos2, offs2, out
+):
+    nc = tc.nc
+    with ExitStack() as ctx:
+        keep = ctx.enter_context(tc.tile_pool(name="keep", bufs=1))
+        bank1 = ctx.enter_context(tc.psum_pool(name="bank1", bufs=5))
+        bank2 = ctx.enter_context(tc.psum_pool(name="bank2", bufs=3))
+
+        slot = {}
+
+        def sb(name, shape, dtype, after=""):
+            slot[name] = slot[after] if after else name
+            return keep.tile(shape, dtype, name=name, tag=slot[name], align_bytes=64)
+
+        offs_t = sb("offs_t", [P, S // 16], U16)
+        offs2_t = sb("offs2_t", [P, S // 16], U16)
+        pos_t = [sb("pos1_t", [P, T // 16], U16), sb("pos2_t", [P, T // 16], U16)]
+        xw = sb("xw", [P, 2 * Q], I32)
+        xs = sb("xs", [P, 2 * Q], U8)
+        xo_raw = [sb("xo_raw%d" % u, [P, 2 * T], F32) for u in range(2)]
+        xo_pair = [sb("xo_pair%d" % u, [P, 2 * T], BF16) for u in range(2)]
+        w1_raw = [sb("w1_raw%d" % g, [P, n * 2 * H], U8) for g, n in enumerate((2, 4))]
+        w1s_raw = sb("w1s_raw", [P, E * H], U8)
+        w1p = {}
+        w1sp = {}
+        w2w = sb("w2w", [P, E * 2 * N], U8)
+        w2s = sb("w2s", [P, E * N], U8)
+        gate_t = [sb("gate%d" % r, [P, T], F32) for r in range(2)]
+        y = [sb("y%d" % b, [P, S], F32) for b in range(2)]
+        warm = sb("warm", [P, 8], F32)
+        warm2 = sb("warm2", [P, 8], F32)
+
+        nc.vector.memset(warm[:], 0.0)
+        nc.vector.memset(w1s_raw[:].bitcast(I32), 0)
+        nc.vector.memset(xw[:, Q:], 0)
+        nc.gpsimd.memset(w2s[:].bitcast(I32), 0)
+        nc.gpsimd.memset(xs[:].bitcast(I32), 0)
+        nc.scalar.activation(warm2[:], warm[:], SILU)
+
+        xo_v = xo.rearrange("(p u j) t -> p u (j t)", u=2, j=2)
+        w1_v = w1_words.bitcast(I32).rearrange("e s p c -> p (e s) c")
+        w2_v = w2_words.bitcast(I32).rearrange("e s p c -> p (e s) c")
+
+        def load_scales(plane, src, width):
+            dst = plane.bitcast(I32).rearrange("p (e c) -> p e c", c=width // 4)
+            rows = src.bitcast(I32)
+            for r in range(4):
+                nc.sync.dma_start(dst[r:P:32], rows[:, r:16:4, :].rearrange("e q c -> q e c"))
+
+        nc.sync.dma_start(offs2_t[:], offs2)
+        nc.sync.dma_start(xw[:, :Q], x_words[0].rearrange("p t d -> p (t d)").bitcast(I32))
+        nc.sync.dma_start(offs_t[:], offs)
+        nc.sync.dma_start(pos_t[0][:], pos1)
+        nc.sync.dma_start(pos_t[1][:], pos2)
+        nc.sync.dma_start(xo_raw[0][:], xo_v[:, 0, :])
+        nc.sync.dma_start(w1_raw[0][:].bitcast(I32).rearrange("p (e c) -> p e c", e=2), w1_v[:, 0:2, :])
+        nc.sync.dma_start(xo_raw[1][:], xo_v[:, 1, :])
+        load_scales(w1s_raw[:], w1_scales.rearrange("e s b i -> (e s) b i"), H)
+        nc.sync.dma_start(w1_raw[1][:].bitcast(I32).rearrange("p (e c) -> p e c", e=4), w1_v[:, 2:6, :])
+        nc.sync.dma_start(w2w[:].bitcast(I32).rearrange("p (e c) -> p e c", e=E), w2_v)
+        load_scales(w2s[:], w2_scales.rearrange("e s b i -> (e s) b i"), N)
+        load_scales(xs[:, :Q], x_scales, Q)
+        for r in range(2):
+            nc.sync.dma_start(gate_t[r][:], gate[r])
+
+        for u in range(2):
+            nc.scalar.copy(
+                xo_pair[u][:].rearrange("p (t j) -> p t j", j=2),
+                xo_raw[u][:].rearrange("p (j t) -> p t j", j=2),
+            )
+
+        def list_cols(e):
+            return slice(e * LIST_COLS, (e + 1) * LIST_COLS)
+
+        rw = [sb("rw%d" % g, [P, 3 * C], U32) for g in range(2)]
+        rs = {}
+
+        def gather_words(g):
+            cols = slice(3 * g * LIST_COLS, 3 * (g + 1) * LIST_COLS)
+            nc.vector.tensor_copy(rw[g][:], xw[:].bitcast(U32).indirect(offs2_t[:, cols]))
+
+        def gather_scales(g):
+            rs[g] = sb("rs%d" % g, [P, 2 * C], U8, after=("halves5", "xq5s", "h5")[g])
+            cols = slice(2 * g * LIST_COLS, 2 * (g + 1) * LIST_COLS)
+            nc.vector.tensor_copy(rs[g][:], xs[:].indirect(offs2_t[:, cols]))
+
+        def permute_w1(e):
+            g, k = (0, e) if e < 2 else (1, e - 2)
+            w1p[e] = sb("w1p%d" % e, [P, 2 * H], U8, after="xq%ds" % (e - 2) if e >= 2 else "")
+            w1sp[e] = sb("w1sp%d" % e, [P, H], U8, after="halves%d" % (e - 1) if e >= 2 else "")
+            raw = w1_raw[g][:, k * 2 * H : (k + 1) * 2 * H].bitcast(U16)
+            nc.vector.tensor_copy(
+                w1p[e][:].bitcast(U16).rearrange("p (t c i) -> p c t i", t=4, i=8),
+                raw.rearrange("p (c i t) -> p c t i", t=4, i=8),
+            )
+            nc.vector.tensor_copy(
+                w1sp[e][:].rearrange("p (t c i) -> p c t i", t=4, i=16),
+                w1s_raw[:, e * H : (e + 1) * H].rearrange("p (c i t) -> p c t i", t=4, i=16),
+            )
+
+        def quantize(name, values, width=C):
+            codes = sb(name + "c", [P, width], U32)
+            scales = sb(name + "s", [P, width], U8)
+            nc.vector.quantize_mx(out=codes[:].bitcast(FP8X4), scales=scales[:], in_=values)
+            return codes[:], scales[:]
+
+        def gather_own(e):
+            halves = sb("halves%d" % e, [P, 2 * C], U32, after="xq%dc" % (e - 2) if e >= 2 else "")
+            for u in range(2):
+                nc.vector.tensor_copy(
+                    halves[:, u * C : (u + 1) * C],
+                    xo_pair[u][:].bitcast(U32).indirect(offs_t[:, list_cols(e)]),
+                )
+            woven = sb("woven%d" % e, [P, 2 * C], U32)
+            nc.scalar.copy(
+                woven[:].rearrange("p (s u) -> p s u", u=2),
+                halves[:].rearrange("p (u s) -> p s u", u=2),
+            )
+            return woven
+
+        def first_layer(hidden, e, codes, scales):
+            for half in range(2):
+                cols = slice(half * P, (half + 1) * P)
+                acc = bank1.tile([P, 4 * P], F32, name="acc1")
+                for t in range(4):
+                    nc.tensor.matmul_mx(
+                        out=acc[:, t * P : (t + 1) * P],
+                        lhsT=w1p[e][:, t * 2 * P : (t + 1) * 2 * P].bitcast(FP4X4),
+                        lhsT_scale=w1sp[e][:, t * P : (t + 1) * P],
+                        rhs=codes[:, cols].bitcast(FP8X4),
+                        rhs_scale=scales[:, cols],
+                        start=True,
+                        stop=True,
+                    )
+                nc.scalar.activation(
+                    hidden[:, half * 4 * P : (half + 1) * 4 * P].rearrange("p (s t) -> p s t", t=4),
+                    acc[:].rearrange("p (t s) -> p s t", t=4),
+                    SILU,
+                )
+
+        def second_layer(e, codes, scales):
+            acc = bank2.tile([P, 2 * C], F32, name="acc2")
+            for b in range(2):
+                col = e * N + b * P
+                nc.tensor.matmul_mx(
+                    out=acc[:, b * C : (b + 1) * C],
+                    lhsT=w2w[:, 2 * col : 2 * (col + P)].bitcast(FP4X4),
+                    lhsT_scale=w2s[:, col : col + P],
+                    rhs=codes.bitcast(FP8X4),
+                    rhs_scale=scales,
+                    start=True,
+                    stop=True,
+                )
+            return acc
+
+        out_v = out.rearrange("(b p) c -> p b c", p=P)
+
+        def finish_own(e, hidden):
+            acc = second_layer(e, *quantize("hq%d" % e, hidden[:]))
+            for b in range(2):
+                nc.scalar.copy(y[b][:, e * C : (e + 1) * C], acc[:, b * C : (b + 1) * C])
+
+        def finish_other(e, codes, scales, after=""):
+            acc = second_layer(e, codes, scales)
+            z = sb("z%d" % e, [P, 2 * C], F32, after=after)
+            nc.scalar.copy(z[:], acc[:])
+            nc.sync.dma_start(
+                out_v[:, :, T + e * C : T + (e + 1) * C], z[:].rearrange("p (b c) -> p b c", b=2)
+            )
+
+        for g in range(2):
+            gather_words(g)
+        permute_w1(0)
+        permute_w1(1)
+
+        woven = {}
+        hidden = {}
+        for step in range(E + 2):
+            if step < E:
+                woven[step] = gather_own(step)
+            if 1 <= step <= E:
+                e = step - 1
+                xq = quantize("xq%d" % e, woven[e][:].bitcast(BF16))
+                hidden[e] = sb("h%d" % e, [P, 4 * C], BF16)
+                first_layer(hidden[e][:], e, *xq)
+                if 2 <= e + 1 < E:
+                    permute_w1(e + 1)
+            if step >= 2:
+                finish_own(step - 2, hidden[step - 2])
+
+        for g in range(3):
+            gather_scales(g)
+
+        hid2 = [sb("g%d" % g, [P, 8 * C], BF16) for g in range(3)]
+
+        def first_other(e):
+            first_layer(
+                hid2[e // 2][:, (e % 2) * 4 * C : (e % 2 + 1) * 4 * C],
+                e,
+                rw[e // 3][:, (e % 3) * C : (e % 3 + 1) * C],
+                rs[e // 2][:, (e % 2) * C : (e % 2 + 1) * C],
+            )
+
+        pieces = [(0, 0, 384), (0, 384, 768), (1, 0, 512), (1, 512, 768)]
+        terms = {}
+        sums = {}
+
+        def product(i, r, term):
+            b, lo, hi = pieces[i]
+            nc.vector.tensor_tensor(
+                term, y[b][:].indirect(pos_t[r][:, lo // 16 : hi // 16]), gate_t[r][:, lo:hi], MULT
+            )
+            terms[i, r] = term
+
+        def total(i, own):
+            b, lo, hi = pieces[i]
+            nc.vector.tensor_tensor(own, terms[i, 0], terms[i, 1], ADD)
+            nc.sync.dma_start(out_v[:, b, lo:hi], own)
+
+        def width(i):
+            return pieces[i][2] - pieces[i][1]
+
+        for e in range(4):
+            first_other(e)
+        for r in range(2):
+            product(0, r, sb("term0_%d" % r, [P, width(0)], F32)[:])
+        for g in range(3):
+            codes, scales = quantize("rq%d" % g, hid2[g][:], 2 * C)
+            if g == 0:
+                first_other(4)
+                first_other(5)
+            for k in range(2):
+                cols = slice(k * C, (k + 1) * C)
+                finish_other(2 * g + k, codes[:, cols], scales[:, cols], after=ZAFTER[2 * g + k])
+            w0, w1 = width(g), width(g + 1)
+            work = sb("work%d" % g, [P, w0 + 2 * w1], F32, after="g%d" % g)
+            product(g + 1, 0, work[:, w0 : w0 + w1])
+            total(g, work[:, :w0])
+            product(g + 1, 1, work[:, w0 + w1 :])
+        total(3, sb("own3", [P, width(3)], F32)[:])

@@ -1,6 +1,7 @@
 from contextlib import ExitStack
 
 import concourse.mybir as mybir
+from concourse.masks import make_identity
 
 K, T, Q, E, C, H, N = 512, 768, 512, 6, 256, 512, 256
 S = E * C
@@ -14,13 +15,20 @@ U16 = mybir.dt.uint16
 U8 = mybir.dt.uint8
 FP8X4 = mybir.dt.float8_e4m3fn_x4
 FP4X4 = mybir.dt.float4_e2m1fn_x4
+COPY = mybir.ActivationFunctionType.Copy
 SILU = mybir.ActivationFunctionType.Silu
 MULT = mybir.AluOpType.mult
 ADD = mybir.AluOpType.add
 
 P = 128
 LIST_COLS = C // 16
-ZAFTER = ("rs1", "", "rs2", "", "", "")
+ZAFTER = ("rs4", "", "", "", "", "")
+RS_PARTS = ((0, 1, "h2"), (1, 2, "halves5"), (2, 4, "h4"), (4, 6, "h5"))
+W1_AFTER = ("", "woven0", "xq1s", "xq2s", "xq3s", "xq4s")
+WEAVE_ON_VECTOR = 6
+HALVES_AFTER = ("", "xo_raw1", "halves0", "halves1", "halves2", "halves3")
+TV = 512
+CAST_SPLIT = 384
 
 
 def tile_moe_loc_mlp_silu_kernel(
@@ -29,8 +37,14 @@ def tile_moe_loc_mlp_silu_kernel(
     nc = tc.nc
     with ExitStack() as ctx:
         keep = ctx.enter_context(tc.tile_pool(name="keep", bufs=1))
-        bank1 = ctx.enter_context(tc.psum_pool(name="bank1", bufs=5))
-        bank2 = ctx.enter_context(tc.psum_pool(name="bank2", bufs=3))
+        psum = ctx.enter_context(tc.psum_pool(name="psum", bufs=1))
+        turns = {"first": 0, "second": 0}
+
+        def bank(role):
+            count = {"first": 5, "second": 3}[role]
+            tag = "%s%d" % (role, turns[role] % count)
+            turns[role] = turns[role] + 1
+            return psum.tile([P, 4 * P], F32, name=tag, tag=tag)
 
         slot = {}
 
@@ -45,23 +59,28 @@ def tile_moe_loc_mlp_silu_kernel(
         xs = sb("xs", [P, 2 * Q], U8)
         xo_raw = [sb("xo_raw%d" % u, [P, 2 * T], F32) for u in range(2)]
         xo_pair = [sb("xo_pair%d" % u, [P, 2 * T], BF16) for u in range(2)]
-        w1_raw = [sb("w1_raw%d" % g, [P, n * 2 * H], U8) for g, n in enumerate((2, 4))]
-        w1s_raw = sb("w1s_raw", [P, E * H], U8)
+        w1_raw = [sb("w1_raw%d" % g, [P, 4 * H], U8) for g in range(3)]
+        w1s_raw = [sb("w1s_raw%d" % g, [P, H], U8) for g in range(2)]
+        ident = sb("ident", [P, P], F32)
+        gate_col = [sb("gate_col%d" % r, [P, 2], F32) for r in range(2)]
         w1p = {}
-        w1sp = {}
+        w1sp = {e: sb("w1sp%d" % e, [P, H], U8) for e in range(E) if e % 4}
         w2w = sb("w2w", [P, E * 2 * N], U8)
         w2s = sb("w2s", [P, E * N], U8)
-        gate_t = [sb("gate%d" % r, [P, T], F32) for r in range(2)]
+        gate_t = [sb("gate%d" % r, [P, TV], F32) for r in range(2)]
         y = [sb("y%d" % b, [P, S], F32) for b in range(2)]
         warm = sb("warm", [P, 8], F32)
         warm2 = sb("warm2", [P, 8], F32)
 
         nc.vector.memset(warm[:], 0.0)
-        nc.vector.memset(w1s_raw[:].bitcast(I32), 0)
         nc.vector.memset(xw[:, Q:], 0)
-        nc.gpsimd.memset(w2s[:].bitcast(I32), 0)
-        nc.gpsimd.memset(xs[:].bitcast(I32), 0)
-        nc.scalar.activation(warm2[:], warm[:], SILU)
+        for g in range(2):
+            nc.gpsimd.memset(w1s_raw[g][:].bitcast(I32), 0)
+        for e in (1, 2, 3, 5):
+            nc.gpsimd.memset(w1sp[e][:].bitcast(I32), 0)
+        nc.vector.memset(w2s[:].bitcast(I32), 0)
+        nc.vector.memset(xs[:].bitcast(I32), 0)
+        make_identity(nc, ident[:])
 
         xo_v = xo.rearrange("(p u j) t -> p u (j t)", u=2, j=2)
         w1_v = w1_words.bitcast(I32).rearrange("e s p c -> p (e s) c")
@@ -73,27 +92,64 @@ def tile_moe_loc_mlp_silu_kernel(
             for r in range(4):
                 nc.sync.dma_start(dst[r:P:32], rows[:, r:16:4, :].rearrange("e q c -> q e c"))
 
+        def load_w1_scales(g):
+            lo, hi = 4 * g, min(4 * g + 4, E)
+            for q in range(4):
+                nc.sync.dma_start(
+                    w1s_raw[g][32 * q : 32 * q + 4 * (hi - lo), :].bitcast(I32),
+                    w1_scales.bitcast(I32)[lo:hi, 0, 4 * q : 4 * q + 4, :],
+                )
+
+        def permute_w1_scales(g, after=""):
+            w1sp[4 * g] = sb("w1sp%d" % (4 * g), [P, H], U8, after=after)
+            nc.vector.tensor_copy(
+                w1sp[4 * g][:].rearrange("p (t c i) -> p c t i", t=4, i=16),
+                w1s_raw[g][:].rearrange("p (c i t) -> p c t i", t=4, i=16),
+            )
+            for e in range(4 * g + 1, min(4 * g + 4, E)):
+                a = 4 * (e % 4)
+                nc.sync.dma_start(w1sp[e][0:112, :].bitcast(I32), w1sp[4 * g][a : a + 112, :].bitcast(I32))
+
+        def load_w1_words(g):
+            nc.sync.dma_start(
+                w1_raw[g][:].bitcast(I32).rearrange("p (e c) -> p e c", e=2), w1_v[:, 2 * g : 2 * g + 2, :]
+            )
+
         nc.sync.dma_start(offs2_t[:], offs2)
-        nc.sync.dma_start(xw[:, :Q], x_words[0].rearrange("p t d -> p (t d)").bitcast(I32))
+        nc.scalar.dma_start(xw[:, :Q], x_words[0].rearrange("p t d -> p (t d)").bitcast(I32))
+        nc.scalar.dma_start(xo_raw[0][:], xo_v[:, 0, :])
+        nc.scalar.dma_start(xo_raw[1][:], xo_v[:, 1, :])
+        nc.scalar.activation(warm2[:], warm[:], SILU)
         nc.sync.dma_start(offs_t[:], offs)
-        nc.sync.dma_start(pos_t[0][:], pos1)
-        nc.sync.dma_start(pos_t[1][:], pos2)
-        nc.sync.dma_start(xo_raw[0][:], xo_v[:, 0, :])
-        nc.sync.dma_start(w1_raw[0][:].bitcast(I32).rearrange("p (e c) -> p e c", e=2), w1_v[:, 0:2, :])
-        nc.sync.dma_start(xo_raw[1][:], xo_v[:, 1, :])
-        load_scales(w1s_raw[:], w1_scales.rearrange("e s b i -> (e s) b i"), H)
-        nc.sync.dma_start(w1_raw[1][:].bitcast(I32).rearrange("p (e c) -> p e c", e=4), w1_v[:, 2:6, :])
+        load_w1_scales(0)
+        load_w1_words(0)
+
+        def cast(engine_copy, u, lo, hi):
+            engine_copy(
+                xo_pair[u][:].rearrange("p (t j) -> p t j", j=2)[:, lo:hi, :],
+                xo_raw[u][:].rearrange("p (j t) -> p t j", j=2)[:, lo:hi, :],
+            )
+
+        cast(nc.scalar.copy, 0, 0, T)
+        cast(nc.scalar.copy, 1, 0, CAST_SPLIT)
+        cast(nc.vector.tensor_copy, 1, CAST_SPLIT, T)
+        permute_w1_scales(0)
+
+        load_w1_words(1)
         nc.sync.dma_start(w2w[:].bitcast(I32).rearrange("p (e c) -> p e c", e=E), w2_v)
         load_scales(w2s[:], w2_scales.rearrange("e s b i -> (e s) b i"), N)
-        load_scales(xs[:, :Q], x_scales, Q)
-        for r in range(2):
-            nc.sync.dma_start(gate_t[r][:], gate[r])
+        load_w1_scales(1)
+        load_w1_words(2)
 
-        for u in range(2):
-            nc.scalar.copy(
-                xo_pair[u][:].rearrange("p (t j) -> p t j", j=2),
-                xo_raw[u][:].rearrange("p (j t) -> p t j", j=2),
-            )
+        def late_loads():
+            load_scales(xs[:, :Q], x_scales, Q)
+            nc.sync.dma_start(pos_t[0][:], pos1)
+            nc.sync.dma_start(pos_t[1][:], pos2)
+            for r in range(2):
+                nc.sync.dma_start(gate_t[r][:], gate[r, :, :TV])
+            with nc.allow_non_contiguous_dma("one weight a token and partition"):
+                for r in range(2):
+                    nc.sync.dma_start(gate_col[r][:], gate[r, 0, TV:].rearrange("(c p) -> p c", p=P))
 
         def list_cols(e):
             return slice(e * LIST_COLS, (e + 1) * LIST_COLS)
@@ -105,23 +161,19 @@ def tile_moe_loc_mlp_silu_kernel(
             cols = slice(3 * g * LIST_COLS, 3 * (g + 1) * LIST_COLS)
             nc.vector.tensor_copy(rw[g][:], xw[:].bitcast(U32).indirect(offs2_t[:, cols]))
 
-        def gather_scales(g):
-            rs[g] = sb("rs%d" % g, [P, 2 * C], U8, after=("halves5", "xq5s", "h5")[g])
-            cols = slice(2 * g * LIST_COLS, 2 * (g + 1) * LIST_COLS)
-            nc.vector.tensor_copy(rs[g][:], xs[:].indirect(offs2_t[:, cols]))
+        def gather_scales(lo, hi, after):
+            part = sb("rs%d" % lo, [P, (hi - lo) * C], U8, after=after)
+            nc.vector.tensor_copy(part[:], xs[:].indirect(offs2_t[:, lo * LIST_COLS : hi * LIST_COLS]))
+            for e in range(lo, hi):
+                rs[e] = part[:, (e - lo) * C : (e - lo + 1) * C]
 
         def permute_w1(e):
-            g, k = (0, e) if e < 2 else (1, e - 2)
-            w1p[e] = sb("w1p%d" % e, [P, 2 * H], U8, after="xq%ds" % (e - 2) if e >= 2 else "")
-            w1sp[e] = sb("w1sp%d" % e, [P, H], U8, after="halves%d" % (e - 1) if e >= 2 else "")
+            g, k = divmod(e, 2)
+            w1p[e] = sb("w1p%d" % e, [P, 2 * H], U8, after=W1_AFTER[e])
             raw = w1_raw[g][:, k * 2 * H : (k + 1) * 2 * H].bitcast(U16)
             nc.vector.tensor_copy(
                 w1p[e][:].bitcast(U16).rearrange("p (t c i) -> p c t i", t=4, i=8),
                 raw.rearrange("p (c i t) -> p c t i", t=4, i=8),
-            )
-            nc.vector.tensor_copy(
-                w1sp[e][:].rearrange("p (t c i) -> p c t i", t=4, i=16),
-                w1s_raw[:, e * H : (e + 1) * H].rearrange("p (c i t) -> p c t i", t=4, i=16),
             )
 
         def quantize(name, values, width=C):
@@ -131,23 +183,32 @@ def tile_moe_loc_mlp_silu_kernel(
             return codes[:], scales[:]
 
         def gather_own(e):
-            halves = sb("halves%d" % e, [P, 2 * C], U32, after="xq%dc" % (e - 2) if e >= 2 else "")
+            halves = sb("halves%d" % e, [P, 2 * C], U32, after=HALVES_AFTER[e])
             for u in range(2):
                 nc.vector.tensor_copy(
                     halves[:, u * C : (u + 1) * C],
                     xo_pair[u][:].bitcast(U32).indirect(offs_t[:, list_cols(e)]),
                 )
-            woven = sb("woven%d" % e, [P, 2 * C], U32)
-            nc.scalar.copy(
-                woven[:].rearrange("p (s u) -> p s u", u=2),
-                halves[:].rearrange("p (u s) -> p s u", u=2),
-            )
+            return halves
+
+        def weave(e, halves):
+            woven = sb("woven%d" % e, [P, 2 * C], U32, after="xq%dc" % (e - 2) if e >= 2 else "")
+            if e < WEAVE_ON_VECTOR:
+                nc.scalar.copy(
+                    woven[:].rearrange("p (s u) -> p s u", u=2),
+                    halves[:].rearrange("p (u s) -> p s u", u=2),
+                )
+            else:
+                nc.vector.tensor_copy(
+                    woven[:].bitcast(I32).rearrange("p (s u) -> p s u", u=2),
+                    halves[:].bitcast(I32).rearrange("p (u s) -> p s u", u=2),
+                )
             return woven
 
         def first_layer(hidden, e, codes, scales):
             for half in range(2):
                 cols = slice(half * P, (half + 1) * P)
-                acc = bank1.tile([P, 4 * P], F32, name="acc1")
+                acc = bank("first")
                 for t in range(4):
                     nc.tensor.matmul_mx(
                         out=acc[:, t * P : (t + 1) * P],
@@ -165,7 +226,7 @@ def tile_moe_loc_mlp_silu_kernel(
                 )
 
         def second_layer(e, codes, scales):
-            acc = bank2.tile([P, 2 * C], F32, name="acc2")
+            acc = bank("second")
             for b in range(2):
                 col = e * N + b * P
                 nc.tensor.matmul_mx(
@@ -196,26 +257,33 @@ def tile_moe_loc_mlp_silu_kernel(
 
         for g in range(2):
             gather_words(g)
-        permute_w1(0)
-        permute_w1(1)
 
         woven = {}
         hidden = {}
-        for step in range(E + 2):
+        picked_halves = {}
+        woven[0] = weave(0, gather_own(0))
+        permute_w1(0)
+        permute_w1(1)
+        woven[1] = weave(1, gather_own(1))
+        for step in range(E + 1):
             if step < E:
-                woven[step] = gather_own(step)
-            if 1 <= step <= E:
-                e = step - 1
-                xq = quantize("xq%d" % e, woven[e][:].bitcast(BF16))
-                hidden[e] = sb("h%d" % e, [P, 4 * C], BF16)
-                first_layer(hidden[e][:], e, *xq)
-                if 2 <= e + 1 < E:
-                    permute_w1(e + 1)
-            if step >= 2:
-                finish_own(step - 2, hidden[step - 2])
-
-        for g in range(3):
-            gather_scales(g)
+                xq = quantize("xq%d" % step, woven[step][:].bitcast(BF16))
+            if step + 2 < E:
+                picked_halves[step + 2] = gather_own(step + 2)
+            if step < E:
+                hidden[step] = sb("h%d" % step, [P, 4 * C], BF16)
+                first_layer(hidden[step][:], step, *xq)
+            if step >= 1:
+                finish_own(step - 1, hidden[step - 1])
+            if 2 <= step + 1 < E:
+                permute_w1(step + 1)
+            if step + 2 < E:
+                woven[step + 2] = weave(step + 2, picked_halves[step + 2])
+            if step == 1:
+                permute_w1_scales(1, after="h0")
+                late_loads()
+        for lo, hi, after in RS_PARTS:
+            gather_scales(lo, hi, after)
 
         hid2 = [sb("g%d" % g, [P, 8 * C], BF16) for g in range(3)]
 
@@ -224,12 +292,47 @@ def tile_moe_loc_mlp_silu_kernel(
                 hid2[e // 2][:, (e % 2) * 4 * C : (e % 2 + 1) * 4 * C],
                 e,
                 rw[e // 3][:, (e % 3) * C : (e % 3 + 1) * C],
-                rs[e // 2][:, (e % 2) * C : (e % 2 + 1) * C],
+                rs[e],
             )
 
-        pieces = [(0, 0, 384), (0, 384, 768), (1, 0, 512), (1, 512, 768)]
+        def turned_gathers():
+            scaled = []
+            for r in range(2):
+                turned = bank("second")
+                for b in range(2):
+                    picked = sb("picked%d_%d" % (r, b), [P, T - TV], F32)
+                    nc.vector.tensor_copy(picked[:], y[b][:].indirect(pos_t[r][:, TV // 16 :]))
+                    for c in range(2):
+                        at = (2 * c + b) * P
+                        nc.tensor.transpose(turned[:, at : at + P], picked[:, c * P : (c + 1) * P], ident[:])
+                weighted = sb("weighted%d" % r, [P, 4 * P], F32)
+                for c in range(2):
+                    cols = slice(2 * c * P, 2 * (c + 1) * P)
+                    nc.scalar.activation(
+                        weighted[:, cols], turned[:, cols], COPY, scale=gate_col[r][:, c : c + 1]
+                    )
+                scaled.append(weighted)
+            return scaled
+
+        def turned_sum(scaled):
+            acc = bank("second")
+            for b in range(2):
+                for c in range(2):
+                    for r in range(2):
+                        nc.tensor.matmul(
+                            acc[:, (2 * b + c) * P : (2 * b + c + 1) * P],
+                            scaled[r][:, (2 * c + b) * P : (2 * c + b + 1) * P],
+                            ident[:],
+                            start=(r == 0),
+                            stop=(r == 1),
+                            is_transpose=True,
+                        )
+            own = sb("own_turned", [P, 4 * P], F32)
+            nc.scalar.copy(own[:], acc[:])
+            nc.sync.dma_start(out_v[:, :, TV:T], own[:].rearrange("p (b c) -> p b c", b=2))
+
+        pieces = [(0, 0, 512), (1, 0, 256), (1, 256, 512)]
         terms = {}
-        sums = {}
 
         def product(i, r, term):
             b, lo, hi = pieces[i]
@@ -246,21 +349,23 @@ def tile_moe_loc_mlp_silu_kernel(
         def width(i):
             return pieces[i][2] - pieces[i][1]
 
-        for e in range(4):
+        for e in range(3):
             first_other(e)
-        for r in range(2):
-            product(0, r, sb("term0_%d" % r, [P, width(0)], F32)[:])
+        scaled = turned_gathers()
+        first_other(3)
+        first_other(4)
+        turned_sum(scaled)
+        first_other(5)
         for g in range(3):
             codes, scales = quantize("rq%d" % g, hid2[g][:], 2 * C)
-            if g == 0:
-                first_other(4)
-                first_other(5)
             for k in range(2):
                 cols = slice(k * C, (k + 1) * C)
                 finish_other(2 * g + k, codes[:, cols], scales[:, cols], after=ZAFTER[2 * g + k])
-            w0, w1 = width(g), width(g + 1)
+            w0 = width(g - 1) if g else 0
+            w1 = width(g)
             work = sb("work%d" % g, [P, w0 + 2 * w1], F32, after="g%d" % g)
-            product(g + 1, 0, work[:, w0 : w0 + w1])
-            total(g, work[:, :w0])
-            product(g + 1, 1, work[:, w0 + w1 :])
-        total(3, sb("own3", [P, width(3)], F32)[:])
+            product(g, 0, work[:, w0 : w0 + w1])
+            if g:
+                total(g - 1, work[:, :w0])
+            product(g, 1, work[:, w0 + w1 :])
+        total(2, sb("own_last", [P, width(2)], F32)[:])

@@ -1,7 +1,6 @@
 from contextlib import ExitStack
 
 import concourse.mybir as mybir
-from concourse.masks import make_identity
 
 K, T, Q, E, C, H, N = 512, 768, 512, 6, 256, 512, 256
 S = E * C
@@ -24,10 +23,10 @@ P = 128
 LIST_COLS = C // 16
 ZAFTER = ("rs4", "", "", "", "", "")
 RS_PARTS = ((0, 1, "h2"), (1, 2, "halves5"), (2, 4, "h4"), (4, 6, "h5"))
-W1_AFTER = ("", "woven0", "xq1s", "xq2s", "xq3s", "xq4s")
+W1_AFTER = ("xo_raw1", "woven0", "xq1s", "xq2s", "xq3s", "xq4s")
 WEAVE_ON_VECTOR = 6
-HALVES_AFTER = ("", "xo_raw1", "halves0", "halves1", "halves2", "halves3")
-TV = 512
+HALVES_AFTER = ("", "", "halves0", "halves1", "halves2", "halves3")
+TV = 768
 CAST_SPLIT = 384
 
 
@@ -61,8 +60,6 @@ def tile_moe_loc_mlp_silu_kernel(
         xo_pair = [sb("xo_pair%d" % u, [P, 2 * T], BF16) for u in range(2)]
         w1_raw = [sb("w1_raw%d" % g, [P, 4 * H], U8) for g in range(3)]
         w1s_raw = [sb("w1s_raw%d" % g, [P, H], U8) for g in range(2)]
-        ident = sb("ident", [P, P], F32)
-        gate_col = [sb("gate_col%d" % r, [P, 2], F32) for r in range(2)]
         w1p = {}
         w1sp = {e: sb("w1sp%d" % e, [P, H], U8) for e in range(E) if e % 4}
         w2w = sb("w2w", [P, E * 2 * N], U8)
@@ -80,7 +77,7 @@ def tile_moe_loc_mlp_silu_kernel(
             nc.gpsimd.memset(w1sp[e][:].bitcast(I32), 0)
         nc.vector.memset(w2s[:].bitcast(I32), 0)
         nc.vector.memset(xs[:].bitcast(I32), 0)
-        make_identity(nc, ident[:])
+
 
         xo_v = xo.rearrange("(p u j) t -> p u (j t)", u=2, j=2)
         w1_v = w1_words.bitcast(I32).rearrange("e s p c -> p (e s) c")
@@ -131,15 +128,15 @@ def tile_moe_loc_mlp_silu_kernel(
             )
 
         cast(nc.scalar.copy, 0, 0, T)
-        cast(nc.scalar.copy, 1, 0, CAST_SPLIT)
-        cast(nc.vector.tensor_copy, 1, CAST_SPLIT, T)
-        permute_w1_scales(0)
+        cast(nc.scalar.copy, 1, 0, T)
 
         load_w1_words(1)
         nc.sync.dma_start(w2w[:].bitcast(I32).rearrange("p (e c) -> p e c", e=E), w2_v)
-        load_scales(w2s[:], w2_scales.rearrange("e s b i -> (e s) b i"), N)
-        load_w1_scales(1)
-        load_w1_words(2)
+
+        def mid_loads():
+            load_scales(w2s[:], w2_scales.rearrange("e s b i -> (e s) b i"), N)
+            load_w1_scales(1)
+            load_w1_words(2)
 
         def late_loads():
             load_scales(xs[:, :Q], x_scales, Q)
@@ -147,9 +144,6 @@ def tile_moe_loc_mlp_silu_kernel(
             nc.sync.dma_start(pos_t[1][:], pos2)
             for r in range(2):
                 nc.sync.dma_start(gate_t[r][:], gate[r, :, :TV])
-            with nc.allow_non_contiguous_dma("one weight a token and partition"):
-                for r in range(2):
-                    nc.sync.dma_start(gate_col[r][:], gate[r, 0, TV:].rearrange("(c p) -> p c", p=P))
 
         def list_cols(e):
             return slice(e * LIST_COLS, (e + 1) * LIST_COLS)
@@ -263,8 +257,10 @@ def tile_moe_loc_mlp_silu_kernel(
         picked_halves = {}
         woven[0] = weave(0, gather_own(0))
         permute_w1(0)
-        permute_w1(1)
         woven[1] = weave(1, gather_own(1))
+        permute_w1_scales(0, after="xo_raw0")
+        permute_w1(1)
+        mid_loads()
         for step in range(E + 1):
             if step < E:
                 xq = quantize("xq%d" % step, woven[step][:].bitcast(BF16))
@@ -295,43 +291,7 @@ def tile_moe_loc_mlp_silu_kernel(
                 rs[e],
             )
 
-        def turned_gathers():
-            scaled = []
-            for r in range(2):
-                turned = bank("second")
-                for b in range(2):
-                    picked = sb("picked%d_%d" % (r, b), [P, T - TV], F32)
-                    nc.vector.tensor_copy(picked[:], y[b][:].indirect(pos_t[r][:, TV // 16 :]))
-                    for c in range(2):
-                        at = (2 * c + b) * P
-                        nc.tensor.transpose(turned[:, at : at + P], picked[:, c * P : (c + 1) * P], ident[:])
-                weighted = sb("weighted%d" % r, [P, 4 * P], F32)
-                for c in range(2):
-                    cols = slice(2 * c * P, 2 * (c + 1) * P)
-                    nc.scalar.activation(
-                        weighted[:, cols], turned[:, cols], COPY, scale=gate_col[r][:, c : c + 1]
-                    )
-                scaled.append(weighted)
-            return scaled
-
-        def turned_sum(scaled):
-            acc = bank("second")
-            for b in range(2):
-                for c in range(2):
-                    for r in range(2):
-                        nc.tensor.matmul(
-                            acc[:, (2 * b + c) * P : (2 * b + c + 1) * P],
-                            scaled[r][:, (2 * c + b) * P : (2 * c + b + 1) * P],
-                            ident[:],
-                            start=(r == 0),
-                            stop=(r == 1),
-                            is_transpose=True,
-                        )
-            own = sb("own_turned", [P, 4 * P], F32)
-            nc.scalar.copy(own[:], acc[:])
-            nc.sync.dma_start(out_v[:, :, TV:T], own[:].rearrange("p (b c) -> p b c", b=2))
-
-        pieces = [(0, 0, 512), (1, 0, 256), (1, 256, 512)]
+        pieces = [(0, 0, 384), (0, 384, 768), (1, 0, 256), (1, 256, 512), (1, 512, 768)]
         terms = {}
 
         def product(i, r, term):
@@ -349,23 +309,22 @@ def tile_moe_loc_mlp_silu_kernel(
         def width(i):
             return pieces[i][2] - pieces[i][1]
 
-        for e in range(3):
+        for e in range(E):
             first_other(e)
-        scaled = turned_gathers()
-        first_other(3)
-        first_other(4)
-        turned_sum(scaled)
-        first_other(5)
+        for r in range(2):
+            product(0, r, sb("term0_%d" % r, [P, width(0)], F32)[:])
         for g in range(3):
             codes, scales = quantize("rq%d" % g, hid2[g][:], 2 * C)
             for k in range(2):
                 cols = slice(k * C, (k + 1) * C)
                 finish_other(2 * g + k, codes[:, cols], scales[:, cols], after=ZAFTER[2 * g + k])
-            w0 = width(g - 1) if g else 0
-            w1 = width(g)
+            w0, w1 = width(g), width(g + 1)
             work = sb("work%d" % g, [P, w0 + 2 * w1], F32, after="g%d" % g)
-            product(g, 0, work[:, w0 : w0 + w1])
-            if g:
-                total(g - 1, work[:, :w0])
-            product(g, 1, work[:, w0 + w1 :])
-        total(2, sb("own_last", [P, width(2)], F32)[:])
+            product(g + 1, 0, work[:, w0 : w0 + w1])
+            total(g, work[:, :w0])
+            product(g + 1, 1, work[:, w0 + w1 :])
+        last = sb("last", [P, 4 * C], F32, after="rq2c")
+        product(4, 0, last[:, :C])
+        total(3, last[:, C : 2 * C])
+        product(4, 1, last[:, 2 * C : 3 * C])
+        total(4, last[:, 3 * C :])

@@ -14,20 +14,24 @@ U16 = mybir.dt.uint16
 U8 = mybir.dt.uint8
 FP8X4 = mybir.dt.float8_e4m3fn_x4
 FP4X4 = mybir.dt.float4_e2m1fn_x4
-COPY = mybir.ActivationFunctionType.Copy
 SILU = mybir.ActivationFunctionType.Silu
 MULT = mybir.AluOpType.mult
 ADD = mybir.AluOpType.add
 
 P = 128
-LIST_COLS = C // 16
-ZAFTER = ("rs4", "", "", "", "", "")
-RS_PARTS = ((0, 1, "h2"), (1, 2, "halves5"), (2, 4, "h4"), (4, 6, "h5"))
-W1_AFTER = ("xo_raw1", "woven0", "xq1s", "xq2s", "xq3s", "xq4s")
-WEAVE_ON_VECTOR = 6
-HALVES_AFTER = ("", "", "halves0", "halves1", "halves2", "halves3")
-TV = 768
-CAST_SPLIT = 384
+PACK = 4
+QUADRANT = 32
+SCALE_ROWS = 16
+PER_COLUMN = 16
+LINE = 16
+ROW_BLOCKS = N // P
+FIRST_BANKS, SECOND_BANKS = 5, 3
+STACK = 4
+MOVED_ROWS = 112
+WINDOW = 2 * Q
+
+PIECES = ((0, 0, 384), (0, 384, 768), (1, 0, 256), (1, 256, 576), (1, 576, 768))
+PAIRS = E // 2
 
 
 def tile_moe_loc_mlp_silu_kernel(
@@ -37,294 +41,277 @@ def tile_moe_loc_mlp_silu_kernel(
     with ExitStack() as ctx:
         keep = ctx.enter_context(tc.tile_pool(name="keep", bufs=1))
         psum = ctx.enter_context(tc.psum_pool(name="psum", bufs=1))
+
         turns = {"first": 0, "second": 0}
 
-        def bank(role):
-            count = {"first": 5, "second": 3}[role]
-            tag = "%s%d" % (role, turns[role] % count)
-            turns[role] = turns[role] + 1
-            return psum.tile([P, 4 * P], F32, name=tag, tag=tag)
+        def bank(layer, count):
+            tag = "%s%d" % (layer, turns[layer] % count)
+            turns[layer] = turns[layer] + 1
+            return psum.tile([P, PACK * P], F32, name=tag, tag=tag)
 
-        slot = {}
+        space = {}
 
-        def sb(name, shape, dtype, after=""):
-            slot[name] = slot[after] if after else name
-            return keep.tile(shape, dtype, name=name, tag=slot[name], align_bytes=64)
+        def sb(name, shape, dtype, reuse=""):
+            space[name] = space[reuse] if reuse else name
+            return keep.tile(shape, dtype, name=name, tag=space[name], align_bytes=64)
 
-        offs_t = sb("offs_t", [P, S // 16], U16)
-        offs2_t = sb("offs2_t", [P, S // 16], U16)
-        pos_t = [sb("pos1_t", [P, T // 16], U16), sb("pos2_t", [P, T // 16], U16)]
-        xw = sb("xw", [P, 2 * Q], I32)
-        xs = sb("xs", [P, 2 * Q], U8)
+        offs_t = sb("offs_t", [P, S // PER_COLUMN], U16)
+        offs2_t = sb("offs2_t", [P, S // PER_COLUMN], U16)
+        pos_t = [sb("pos1_t", [P, T // PER_COLUMN], U16), sb("pos2_t", [P, T // PER_COLUMN], U16)]
+        other_words = sb("other_words", [P, WINDOW], I32)
+        other_plane = sb("other_plane", [P, WINDOW], U8)
         xo_raw = [sb("xo_raw%d" % u, [P, 2 * T], F32) for u in range(2)]
-        xo_pair = [sb("xo_pair%d" % u, [P, 2 * T], BF16) for u in range(2)]
-        w1_raw = [sb("w1_raw%d" % g, [P, 4 * H], U8) for g in range(3)]
-        w1s_raw = [sb("w1s_raw%d" % g, [P, H], U8) for g in range(2)]
-        w1p = {}
-        w1sp = {e: sb("w1sp%d" % e, [P, H], U8) for e in range(E) if e % 4}
-        w2w = sb("w2w", [P, E * 2 * N], U8)
-        w2s = sb("w2s", [P, E * N], U8)
-        gate_t = [sb("gate%d" % r, [P, TV], F32) for r in range(2)]
-        y = [sb("y%d" % b, [P, S], F32) for b in range(2)]
-        warm = sb("warm", [P, 8], F32)
-        warm2 = sb("warm2", [P, 8], F32)
+        xo_pairs = [sb("xo_pairs%d" % u, [P, 2 * T], BF16) for u in range(2)]
+        w1_raw = [sb("w1_raw%d" % g, [P, 2 * 2 * H], U8) for g in range(PAIRS)]
+        w1_stack = [sb("w1_stack%d" % g, [P, H], U8) for g in range(2)]
+        w1_perm = {}
+        w1_plane = {e: sb("w1_plane%d" % e, [P, H], U8) for e in range(E) if e % STACK}
+        w2_all = sb("w2_all", [P, E * 2 * N], U8)
+        w2_plane = sb("w2_plane", [P, E * N], U8)
+        gate_t = [sb("gate%d" % r, [P, T], F32) for r in range(2)]
+        y = [sb("y%d" % b, [P, S], F32) for b in range(ROW_BLOCKS)]
+        warm_in = sb("warm_in", [P, 8], F32)
+        warm_out = sb("warm_out", [P, 8], F32)
 
-        nc.vector.memset(warm[:], 0.0)
-        nc.vector.memset(xw[:, Q:], 0)
-        for g in range(2):
-            nc.gpsimd.memset(w1s_raw[g][:].bitcast(I32), 0)
-        for e in (1, 2, 3, 5):
-            nc.gpsimd.memset(w1sp[e][:].bitcast(I32), 0)
-        nc.vector.memset(w2s[:].bitcast(I32), 0)
-        nc.vector.memset(xs[:].bitcast(I32), 0)
+        nc.vector.memset(warm_in[:], 0.0)
+        nc.vector.memset(other_words[:, Q:], 0)
+        for stack in w1_stack:
+            nc.gpsimd.memset(stack[:].bitcast(I32), 0)
+        for e in sorted(w1_plane):
+            nc.gpsimd.memset(w1_plane[e][:].bitcast(I32), 0)
+        nc.vector.memset(w2_plane[:].bitcast(I32), 0)
+        nc.vector.memset(other_plane[:].bitcast(I32), 0)
 
+        xo_halves = xo.rearrange("(p u j) t -> p u (j t)", u=2, j=2)
+        w1_rows = w1_words.bitcast(I32).rearrange("e s p c -> p (e s) c")
+        w2_rows = w2_words.bitcast(I32).rearrange("e s p c -> p (e s) c")
+        out_rows = out.rearrange("(b p) c -> p b c", p=P)
 
-        xo_v = xo.rearrange("(p u j) t -> p u (j t)", u=2, j=2)
-        w1_v = w1_words.bitcast(I32).rearrange("e s p c -> p (e s) c")
-        w2_v = w2_words.bitcast(I32).rearrange("e s p c -> p (e s) c")
+        def load_plane(plane, scales, width):
+            dst = plane.bitcast(I32).rearrange("p (m c) -> p m c", c=width // 4)
+            rows = scales.bitcast(I32)
+            for r in range(PACK):
+                nc.sync.dma_start(dst[r:P:QUADRANT], rows[:, r:SCALE_ROWS:PACK, :].rearrange("m q c -> q m c"))
 
-        def load_scales(plane, src, width):
-            dst = plane.bitcast(I32).rearrange("p (e c) -> p e c", c=width // 4)
-            rows = src.bitcast(I32)
-            for r in range(4):
-                nc.sync.dma_start(dst[r:P:32], rows[:, r:16:4, :].rearrange("e q c -> q e c"))
-
-        def load_w1_scales(g):
-            lo, hi = 4 * g, min(4 * g + 4, E)
-            for q in range(4):
+        def load_w1_stack(g):
+            lo, hi = STACK * g, min(STACK * (g + 1), E)
+            for q in range(P // QUADRANT):
                 nc.sync.dma_start(
-                    w1s_raw[g][32 * q : 32 * q + 4 * (hi - lo), :].bitcast(I32),
-                    w1_scales.bitcast(I32)[lo:hi, 0, 4 * q : 4 * q + 4, :],
+                    w1_stack[g][QUADRANT * q : QUADRANT * q + PACK * (hi - lo), :].bitcast(I32),
+                    w1_scales.bitcast(I32)[lo:hi, 0, PACK * q : PACK * (q + 1), :],
                 )
-
-        def permute_w1_scales(g, after=""):
-            w1sp[4 * g] = sb("w1sp%d" % (4 * g), [P, H], U8, after=after)
-            nc.vector.tensor_copy(
-                w1sp[4 * g][:].rearrange("p (t c i) -> p c t i", t=4, i=16),
-                w1s_raw[g][:].rearrange("p (c i t) -> p c t i", t=4, i=16),
-            )
-            for e in range(4 * g + 1, min(4 * g + 4, E)):
-                a = 4 * (e % 4)
-                nc.sync.dma_start(w1sp[e][0:112, :].bitcast(I32), w1sp[4 * g][a : a + 112, :].bitcast(I32))
 
         def load_w1_words(g):
             nc.sync.dma_start(
-                w1_raw[g][:].bitcast(I32).rearrange("p (e c) -> p e c", e=2), w1_v[:, 2 * g : 2 * g + 2, :]
+                w1_raw[g][:].bitcast(I32).rearrange("p (e c) -> p e c", e=2), w1_rows[:, 2 * g : 2 * g + 2, :]
             )
 
-        nc.sync.dma_start(offs2_t[:], offs2)
-        nc.scalar.dma_start(xw[:, :Q], x_words[0].rearrange("p t d -> p (t d)").bitcast(I32))
-        nc.scalar.dma_start(xo_raw[0][:], xo_v[:, 0, :])
-        nc.scalar.dma_start(xo_raw[1][:], xo_v[:, 1, :])
-        nc.scalar.activation(warm2[:], warm[:], SILU)
-        nc.sync.dma_start(offs_t[:], offs)
-        load_w1_scales(0)
-        load_w1_words(0)
-
-        def cast(engine_copy, u, lo, hi):
-            engine_copy(
-                xo_pair[u][:].rearrange("p (t j) -> p t j", j=2)[:, lo:hi, :],
-                xo_raw[u][:].rearrange("p (j t) -> p t j", j=2)[:, lo:hi, :],
-            )
-
-        cast(nc.scalar.copy, 0, 0, T)
-        cast(nc.scalar.copy, 1, 0, T)
-
-        load_w1_words(1)
-        nc.sync.dma_start(w2w[:].bitcast(I32).rearrange("p (e c) -> p e c", e=E), w2_v)
-
-        def mid_loads():
-            load_scales(w2s[:], w2_scales.rearrange("e s b i -> (e s) b i"), N)
-            load_w1_scales(1)
-            load_w1_words(2)
-
-        def late_loads():
-            load_scales(xs[:, :Q], x_scales, Q)
-            nc.sync.dma_start(pos_t[0][:], pos1)
-            nc.sync.dma_start(pos_t[1][:], pos2)
-            for r in range(2):
-                nc.sync.dma_start(gate_t[r][:], gate[r, :, :TV])
-
-        def list_cols(e):
-            return slice(e * LIST_COLS, (e + 1) * LIST_COLS)
-
-        rw = [sb("rw%d" % g, [P, 3 * C], U32) for g in range(2)]
-        rs = {}
-
-        def gather_words(g):
-            cols = slice(3 * g * LIST_COLS, 3 * (g + 1) * LIST_COLS)
-            nc.vector.tensor_copy(rw[g][:], xw[:].bitcast(U32).indirect(offs2_t[:, cols]))
-
-        def gather_scales(lo, hi, after):
-            part = sb("rs%d" % lo, [P, (hi - lo) * C], U8, after=after)
-            nc.vector.tensor_copy(part[:], xs[:].indirect(offs2_t[:, lo * LIST_COLS : hi * LIST_COLS]))
-            for e in range(lo, hi):
-                rs[e] = part[:, (e - lo) * C : (e - lo + 1) * C]
-
-        def permute_w1(e):
-            g, k = divmod(e, 2)
-            w1p[e] = sb("w1p%d" % e, [P, 2 * H], U8, after=W1_AFTER[e])
-            raw = w1_raw[g][:, k * 2 * H : (k + 1) * 2 * H].bitcast(U16)
+        def permute_columns(dst, src, run):
             nc.vector.tensor_copy(
-                w1p[e][:].bitcast(U16).rearrange("p (t c i) -> p c t i", t=4, i=8),
-                raw.rearrange("p (c i t) -> p c t i", t=4, i=8),
+                dst.rearrange("p (t c i) -> p c t i", t=PACK, i=run),
+                src.rearrange("p (c i t) -> p c t i", t=PACK, i=run),
             )
 
-        def quantize(name, values, width=C):
-            codes = sb(name + "c", [P, width], U32)
-            scales = sb(name + "s", [P, width], U8)
-            nc.vector.quantize_mx(out=codes[:].bitcast(FP8X4), scales=scales[:], in_=values)
-            return codes[:], scales[:]
+        def permute_w1_stack(g, reuse):
+            first = STACK * g
+            w1_plane[first] = sb("w1_plane%d" % first, [P, H], U8, reuse=reuse)
+            permute_columns(w1_plane[first][:], w1_stack[g][:], LINE)
+            for e in range(first + 1, min(first + STACK, E)):
+                place = PACK * (e - first)
+                nc.sync.dma_start(
+                    w1_plane[e][0:MOVED_ROWS, :].bitcast(I32),
+                    w1_plane[first][place : place + MOVED_ROWS, :].bitcast(I32),
+                )
+
+        def permute_w1_words(e, reuse):
+            pair, k = divmod(e, 2)
+            w1_perm[e] = sb("w1_perm%d" % e, [P, 2 * H], U8, reuse=reuse)
+            raw = w1_raw[pair][:, k * 2 * H : (k + 1) * 2 * H]
+            permute_columns(w1_perm[e][:].bitcast(U16), raw.bitcast(U16), LINE // 2)
+
+        def list_columns(lo, hi):
+            return slice(lo // PER_COLUMN, hi // PER_COLUMN)
+
+        def quantize(name, values, width):
+            codes = sb(name + "_codes", [P, width], U32)
+            plane = sb(name + "_plane", [P, width], U8)
+            nc.vector.quantize_mx(out=codes[:].bitcast(FP8X4), scales=plane[:], in_=values)
+            return codes[:], plane[:]
 
         def gather_own(e):
-            halves = sb("halves%d" % e, [P, 2 * C], U32, after=HALVES_AFTER[e])
+            halves = sb("halves%d" % e, [P, 2 * C], U32, reuse="halves%d" % (e - 2) if e >= 2 else "")
             for u in range(2):
                 nc.vector.tensor_copy(
                     halves[:, u * C : (u + 1) * C],
-                    xo_pair[u][:].bitcast(U32).indirect(offs_t[:, list_cols(e)]),
+                    xo_pairs[u][:].bitcast(U32).indirect(offs_t[:, list_columns(e * C, (e + 1) * C)]),
                 )
             return halves
 
         def weave(e, halves):
-            woven = sb("woven%d" % e, [P, 2 * C], U32, after="xq%dc" % (e - 2) if e >= 2 else "")
-            if e < WEAVE_ON_VECTOR:
-                nc.scalar.copy(
-                    woven[:].rearrange("p (s u) -> p s u", u=2),
-                    halves[:].rearrange("p (u s) -> p s u", u=2),
-                )
-            else:
-                nc.vector.tensor_copy(
-                    woven[:].bitcast(I32).rearrange("p (s u) -> p s u", u=2),
-                    halves[:].bitcast(I32).rearrange("p (u s) -> p s u", u=2),
-                )
+            woven = sb("woven%d" % e, [P, 2 * C], U32, reuse="x%d_codes" % (e - 2) if e >= 2 else "")
+            nc.scalar.copy(
+                woven[:].rearrange("p (s u) -> p s u", u=2),
+                halves[:].rearrange("p (u s) -> p s u", u=2),
+            )
             return woven
 
-        def first_layer(hidden, e, codes, scales):
-            for half in range(2):
-                cols = slice(half * P, (half + 1) * P)
-                acc = bank("first")
-                for t in range(4):
+        def first_layer(hidden, e, codes, plane):
+            for block in range(C // P):
+                cols = slice(block * P, (block + 1) * P)
+                acc = bank("first", FIRST_BANKS)
+                for t in range(PACK):
                     nc.tensor.matmul_mx(
                         out=acc[:, t * P : (t + 1) * P],
-                        lhsT=w1p[e][:, t * 2 * P : (t + 1) * 2 * P].bitcast(FP4X4),
-                        lhsT_scale=w1sp[e][:, t * P : (t + 1) * P],
+                        lhsT=w1_perm[e][:, t * 2 * P : (t + 1) * 2 * P].bitcast(FP4X4),
+                        lhsT_scale=w1_plane[e][:, t * P : (t + 1) * P],
                         rhs=codes[:, cols].bitcast(FP8X4),
-                        rhs_scale=scales[:, cols],
+                        rhs_scale=plane[:, cols],
                         start=True,
                         stop=True,
                     )
                 nc.scalar.activation(
-                    hidden[:, half * 4 * P : (half + 1) * 4 * P].rearrange("p (s t) -> p s t", t=4),
-                    acc[:].rearrange("p (t s) -> p s t", t=4),
+                    hidden[:, block * PACK * P : (block + 1) * PACK * P].rearrange("p (s t) -> p s t", t=PACK),
+                    acc[:].rearrange("p (t s) -> p s t", t=PACK),
                     SILU,
                 )
 
-        def second_layer(e, codes, scales):
-            acc = bank("second")
-            for b in range(2):
+        def second_layer(e, codes, plane):
+            acc = bank("second", SECOND_BANKS)
+            for b in range(ROW_BLOCKS):
                 col = e * N + b * P
                 nc.tensor.matmul_mx(
                     out=acc[:, b * C : (b + 1) * C],
-                    lhsT=w2w[:, 2 * col : 2 * (col + P)].bitcast(FP4X4),
-                    lhsT_scale=w2s[:, col : col + P],
+                    lhsT=w2_all[:, 2 * col : 2 * (col + P)].bitcast(FP4X4),
+                    lhsT_scale=w2_plane[:, col : col + P],
                     rhs=codes.bitcast(FP8X4),
-                    rhs_scale=scales,
+                    rhs_scale=plane,
                     start=True,
                     stop=True,
                 )
             return acc
 
-        out_v = out.rearrange("(b p) c -> p b c", p=P)
+        nc.sync.dma_start(offs2_t[:], offs2)
+        nc.scalar.dma_start(other_words[:, :Q], x_words[0].rearrange("p t d -> p (t d)").bitcast(I32))
+        for u in range(2):
+            nc.scalar.dma_start(xo_raw[u][:], xo_halves[:, u, :])
+        nc.scalar.activation(warm_out[:], warm_in[:], SILU)
+        nc.sync.dma_start(offs_t[:], offs)
+        load_w1_stack(0)
+        load_w1_words(0)
 
-        def finish_own(e, hidden):
-            acc = second_layer(e, *quantize("hq%d" % e, hidden[:]))
-            for b in range(2):
-                nc.scalar.copy(y[b][:, e * C : (e + 1) * C], acc[:, b * C : (b + 1) * C])
-
-        def finish_other(e, codes, scales, after=""):
-            acc = second_layer(e, codes, scales)
-            z = sb("z%d" % e, [P, 2 * C], F32, after=after)
-            nc.scalar.copy(z[:], acc[:])
-            nc.sync.dma_start(
-                out_v[:, :, T + e * C : T + (e + 1) * C], z[:].rearrange("p (b c) -> p b c", b=2)
+        for u in range(2):
+            nc.scalar.copy(
+                xo_pairs[u][:].rearrange("p (t j) -> p t j", j=2),
+                xo_raw[u][:].rearrange("p (j t) -> p t j", j=2),
             )
 
+        load_w1_words(1)
+        nc.sync.dma_start(w2_all[:].bitcast(I32).rearrange("p (e c) -> p e c", e=E), w2_rows)
+
+        picked_words = [sb("picked_words%d" % g, [P, S // 2], U32) for g in range(2)]
         for g in range(2):
-            gather_words(g)
+            entries = offs2_t[:, list_columns(g * S // 2, (g + 1) * S // 2)]
+            nc.vector.tensor_copy(picked_words[g][:], other_words[:].bitcast(U32).indirect(entries))
 
-        woven = {}
-        hidden = {}
-        picked_halves = {}
-        woven[0] = weave(0, gather_own(0))
-        permute_w1(0)
+        woven = {0: weave(0, gather_own(0))}
+        permute_w1_words(0, reuse="xo_raw1")
         woven[1] = weave(1, gather_own(1))
-        permute_w1_scales(0, after="xo_raw0")
-        permute_w1(1)
-        mid_loads()
-        for step in range(E + 1):
-            if step < E:
-                xq = quantize("xq%d" % step, woven[step][:].bitcast(BF16))
-            if step + 2 < E:
-                picked_halves[step + 2] = gather_own(step + 2)
-            if step < E:
-                hidden[step] = sb("h%d" % step, [P, 4 * C], BF16)
-                first_layer(hidden[step][:], step, *xq)
-            if step >= 1:
-                finish_own(step - 1, hidden[step - 1])
-            if 2 <= step + 1 < E:
-                permute_w1(step + 1)
-            if step + 2 < E:
-                woven[step + 2] = weave(step + 2, picked_halves[step + 2])
-            if step == 1:
-                permute_w1_scales(1, after="h0")
-                late_loads()
-        for lo, hi, after in RS_PARTS:
-            gather_scales(lo, hi, after)
+        permute_w1_stack(0, reuse="xo_raw0")
+        permute_w1_words(1, reuse="woven0")
+        load_plane(w2_plane[:], w2_scales.rearrange("e s b n -> (e s) b n"), N)
+        load_w1_stack(1)
+        load_w1_words(2)
 
-        hid2 = [sb("g%d" % g, [P, 8 * C], BF16) for g in range(3)]
+        hidden = {}
+        for e in range(E + 1):
+            if e < E:
+                x_codes, x_plane = quantize("x%d" % e, woven[e][:].bitcast(BF16), C)
+            if e + 2 < E:
+                halves = gather_own(e + 2)
+            if e < E:
+                hidden[e] = sb("hidden%d" % e, [P, PACK * C], BF16)
+                first_layer(hidden[e][:], e, x_codes, x_plane)
+            if e >= 1:
+                acc = second_layer(e - 1, *quantize("h%d" % (e - 1), hidden[e - 1][:], C))
+                for b in range(ROW_BLOCKS):
+                    nc.scalar.copy(y[b][:, (e - 1) * C : e * C], acc[:, b * C : (b + 1) * C])
+            if 2 <= e + 1 < E:
+                permute_w1_words(e + 1, reuse="x%d_plane" % e)
+            if e + 2 < E:
+                woven[e + 2] = weave(e + 2, halves)
+            if e == 1:
+                permute_w1_stack(1, reuse="hidden0")
+                load_plane(other_plane[:, :Q], x_scales, Q)
+                nc.sync.dma_start(pos_t[0][:], pos1)
+                nc.sync.dma_start(pos_t[1][:], pos2)
+                for r in range(2):
+                    nc.sync.dma_start(gate_t[r][:], gate[r])
 
-        def first_other(e):
-            first_layer(
-                hid2[e // 2][:, (e % 2) * 4 * C : (e % 2 + 1) * 4 * C],
-                e,
-                rw[e // 3][:, (e % 3) * C : (e % 3 + 1) * C],
-                rs[e],
-            )
+        picked_plane = {}
+        last = E - 1
+        for lo, hi, reuse in (
+            (0, 1, "hidden2"),
+            (1, 2, "halves%d" % last),
+            (2, 4, "hidden%d" % (last - 1)),
+            (4, E, "hidden%d" % last),
+        ):
+            part = sb("picked_plane%d" % lo, [P, (hi - lo) * C], U8, reuse=reuse)
+            nc.vector.tensor_copy(part[:], other_plane[:].indirect(offs2_t[:, list_columns(lo * C, hi * C)]))
+            for e in range(lo, hi):
+                picked_plane[e] = part[:, (e - lo) * C : (e - lo + 1) * C]
 
-        pieces = [(0, 0, 384), (0, 384, 768), (1, 0, 256), (1, 256, 512), (1, 512, 768)]
-        terms = {}
-
-        def product(i, r, term):
-            b, lo, hi = pieces[i]
-            nc.vector.tensor_tensor(
-                term, y[b][:].indirect(pos_t[r][:, lo // 16 : hi // 16]), gate_t[r][:, lo:hi], MULT
-            )
-            terms[i, r] = term
-
-        def total(i, own):
-            b, lo, hi = pieces[i]
-            nc.vector.tensor_tensor(own, terms[i, 0], terms[i, 1], ADD)
-            nc.sync.dma_start(out_v[:, b, lo:hi], own)
-
-        def width(i):
-            return pieces[i][2] - pieces[i][1]
-
+        pair_hidden = [sb("pair_hidden%d" % g, [P, 2 * PACK * C], BF16) for g in range(PAIRS)]
         for e in range(E):
-            first_other(e)
-        for r in range(2):
-            product(0, r, sb("term0_%d" % r, [P, width(0)], F32)[:])
-        for g in range(3):
-            codes, scales = quantize("rq%d" % g, hid2[g][:], 2 * C)
+            half, k = divmod(e, E // 2)
+            first_layer(
+                pair_hidden[e // 2][:, (e % 2) * PACK * C : (e % 2 + 1) * PACK * C],
+                e,
+                picked_words[half][:, k * C : (k + 1) * C],
+                picked_plane[e],
+            )
+
+        def finish_pair(g):
+            codes, plane = quantize("pair%d" % g, pair_hidden[g][:], 2 * C)
             for k in range(2):
-                cols = slice(k * C, (k + 1) * C)
-                finish_other(2 * g + k, codes[:, cols], scales[:, cols], after=ZAFTER[2 * g + k])
-            w0, w1 = width(g), width(g + 1)
-            work = sb("work%d" % g, [P, w0 + 2 * w1], F32, after="g%d" % g)
-            product(g + 1, 0, work[:, w0 : w0 + w1])
-            total(g, work[:, :w0])
-            product(g + 1, 1, work[:, w0 + w1 :])
-        last = sb("last", [P, 4 * C], F32, after="rq2c")
-        product(4, 0, last[:, :C])
-        total(3, last[:, C : 2 * C])
-        product(4, 1, last[:, 2 * C : 3 * C])
-        total(4, last[:, 3 * C :])
+                e = 2 * g + k
+                acc = second_layer(e, codes[:, k * C : (k + 1) * C], plane[:, k * C : (k + 1) * C])
+                z = sb("z%d" % e, [P, ROW_BLOCKS * C], F32, reuse="picked_plane4" if e == 0 else "")
+                nc.scalar.copy(z[:], acc[:])
+                nc.sync.dma_start(
+                    out_rows[:, :, T + e * C : T + (e + 1) * C], z[:].rearrange("p (b c) -> p b c", b=ROW_BLOCKS)
+                )
+
+        widths = [hi - lo for b, lo, hi in PIECES]
+        work = {}
+
+        def product(i, r):
+            b, lo, hi = PIECES[i]
+            nc.vector.tensor_tensor(
+                work[i][:, r * widths[i] : (r + 1) * widths[i]],
+                y[b][:].indirect(pos_t[r][:, list_columns(lo, hi)]),
+                gate_t[r][:, lo:hi],
+                MULT,
+            )
+
+        def add_and_store(i):
+            b, lo, hi = PIECES[i]
+            w = widths[i]
+            nc.vector.tensor_tensor(work[i][:, 2 * w :], work[i][:, :w], work[i][:, w : 2 * w], ADD)
+            nc.sync.dma_start(out_rows[:, b, lo:hi], work[i][:, 2 * w :])
+
+        for i in range(len(PIECES) + 1):
+            if 1 <= i <= PAIRS:
+                finish_pair(i - 1)
+            if i < PAIRS:
+                work[i] = sb("work%d" % i, [P, 3 * widths[i]], F32)[:]
+            elif i == PAIRS:
+                tail = sb("tail", [P, 3 * sum(widths[PAIRS:])], F32, reuse="pair_hidden%d" % (PAIRS - 1))
+                for j in range(PAIRS, len(PIECES)):
+                    at = 3 * sum(widths[PAIRS:j])
+                    work[j] = tail[:, at : at + 3 * widths[j]]
+            if i < len(PIECES):
+                product(i, 0)
+            if i >= 1:
+                add_and_store(i - 1)
+            if i < len(PIECES):
+                product(i, 1)

@@ -70,10 +70,7 @@ def tile_moe_loc_mlp_silu_kernel(
         w2_plane = sb("w2_plane", [P, E * N], U8)
         gate_t = [sb("gate%d" % r, [P, T], F32) for r in range(2)]
         y = [sb("y%d" % b, [P, S], F32) for b in range(ROW_BLOCKS)]
-        warm_in = sb("warm_in", [P, 8], F32)
-        warm_out = sb("warm_out", [P, 8], F32)
 
-        nc.vector.memset(warm_in[:], 0.0)
         nc.vector.memset(other_words[:, Q:], 0)
         for stack in w1_stack:
             nc.gpsimd.memset(stack[:].bitcast(I32), 0)
@@ -194,7 +191,6 @@ def tile_moe_loc_mlp_silu_kernel(
         nc.scalar.dma_start(other_words[:, :Q], x_words[0].rearrange("p t d -> p (t d)").bitcast(I32))
         for u in range(2):
             nc.scalar.dma_start(xo_raw[u][:], xo_halves[:, u, :])
-        nc.scalar.activation(warm_out[:], warm_in[:], SILU)
         nc.sync.dma_start(offs_t[:], offs)
         load_w1_stack(0)
         load_w1_words(0)

@@ -30,7 +30,7 @@ STACK = 4
 MOVED_ROWS = 112
 WINDOW = 2 * Q
 
-PIECES = ((0, 0, 384), (0, 384, 768), (1, 0, 256), (1, 256, 576), (1, 576, 768))
+PIECES = ((0, 0, 384), (0, 384, 768), (1, 0, 320), (1, 320, 640), (1, 640, 768))
 PAIRS = E // 2
 
 
@@ -232,11 +232,11 @@ def tile_moe_loc_mlp_silu_kernel(
                 for b in range(ROW_BLOCKS):
                     nc.scalar.copy(y[b][:, (e - 1) * C : e * C], acc[:, b * C : (b + 1) * C])
             if 2 <= e + 1 < E:
-                permute_w1_words(e + 1, reuse="x%d_plane" % e)
+                permute_w1_words(e + 1, reuse="x%d_plane" % (e - 1))
             if e + 2 < E:
                 woven[e + 2] = weave(e + 2, halves)
             if e == 1:
-                permute_w1_stack(1, reuse="hidden0")
+                permute_w1_stack(1, reuse="woven1")
                 load_plane(other_plane[:, :Q], x_scales, Q)
                 nc.sync.dma_start(pos_t[0][:], pos1)
                 nc.sync.dma_start(pos_t[1][:], pos2)
@@ -257,33 +257,50 @@ def tile_moe_loc_mlp_silu_kernel(
                 picked_plane[e] = part[:, (e - lo) * C : (e - lo + 1) * C]
 
         pair_hidden = [sb("pair_hidden%d" % g, [P, 2 * PACK * C], BF16) for g in range(PAIRS)]
-        for e in range(E):
-            half, k = divmod(e, E // 2)
-            first_layer(
-                pair_hidden[e // 2][:, (e % 2) * PACK * C : (e % 2 + 1) * PACK * C],
-                e,
-                picked_words[half][:, k * C : (k + 1) * C],
-                picked_plane[e],
-            )
+
+        def start_pair(g):
+            for e in (2 * g, 2 * g + 1):
+                half, k = divmod(e, E // 2)
+                first_layer(
+                    pair_hidden[g][:, (e % 2) * PACK * C : (e % 2 + 1) * PACK * C],
+                    e,
+                    picked_words[half][:, k * C : (k + 1) * C],
+                    picked_plane[e],
+                )
+
+        start_pair(0)
+        start_pair(1)
 
         def finish_pair(g):
             codes, plane = quantize("pair%d" % g, pair_hidden[g][:], 2 * C)
             for k in range(2):
                 e = 2 * g + k
                 acc = second_layer(e, codes[:, k * C : (k + 1) * C], plane[:, k * C : (k + 1) * C])
-                z = sb("z%d" % e, [P, ROW_BLOCKS * C], F32, reuse="picked_plane4" if e == 0 else "")
+                z = sb("z%d" % e, [P, ROW_BLOCKS * C], F32, reuse="")
                 nc.scalar.copy(z[:], acc[:])
                 nc.sync.dma_start(
                     out_rows[:, :, T + e * C : T + (e + 1) * C], z[:].rearrange("p (b c) -> p b c", b=ROW_BLOCKS)
                 )
 
         widths = [hi - lo for b, lo, hi in PIECES]
-        work = {}
+        products = {}
+        sums = {}
+
+        def stage(name, done, todo, last_sums, reuse=""):
+            total = sum(widths[i] for i in done + last_sums) + 2 * sum(widths[i] for i in todo)
+            space_of = sb(name, [P, total], F32, reuse=reuse)
+            at = 0
+            for i in done + last_sums:
+                sums[i] = space_of[:, at : at + widths[i]]
+                at = at + widths[i]
+            for i in todo:
+                products[i] = space_of[:, at : at + 2 * widths[i]]
+                at = at + 2 * widths[i]
 
         def product(i, r):
             b, lo, hi = PIECES[i]
             nc.vector.tensor_tensor(
-                work[i][:, r * widths[i] : (r + 1) * widths[i]],
+                products[i][:, r * widths[i] : (r + 1) * widths[i]],
                 y[b][:].indirect(pos_t[r][:, list_columns(lo, hi)]),
                 gate_t[r][:, lo:hi],
                 MULT,
@@ -292,22 +309,26 @@ def tile_moe_loc_mlp_silu_kernel(
         def add_and_store(i):
             b, lo, hi = PIECES[i]
             w = widths[i]
-            nc.vector.tensor_tensor(work[i][:, 2 * w :], work[i][:, :w], work[i][:, w : 2 * w], ADD)
-            nc.sync.dma_start(out_rows[:, b, lo:hi], work[i][:, 2 * w :])
+            nc.vector.tensor_tensor(sums[i], products[i][:, :w], products[i][:, w:], ADD)
+            nc.sync.dma_start(out_rows[:, b, lo:hi], sums[i])
 
-        for i in range(len(PIECES) + 1):
-            if 1 <= i <= PAIRS:
-                finish_pair(i - 1)
-            if i < PAIRS:
-                work[i] = sb("work%d" % i, [P, 3 * widths[i]], F32)[:]
-            elif i == PAIRS:
-                tail = sb("tail", [P, 3 * sum(widths[PAIRS:])], F32, reuse="pair_hidden%d" % (PAIRS - 1))
-                for j in range(PAIRS, len(PIECES)):
-                    at = 3 * sum(widths[PAIRS:j])
-                    work[j] = tail[:, at : at + 3 * widths[j]]
-            if i < len(PIECES):
-                product(i, 0)
-            if i >= 1:
-                add_and_store(i - 1)
-            if i < len(PIECES):
-                product(i, 1)
+        stage("stage0", [], [0], [])
+        product(0, 0)
+        product(0, 1)
+        for g in range(PAIRS):
+            finish_pair(g)
+            if g == 0:
+                start_pair(2)
+            if g < PAIRS - 1:
+                stage("stage%d" % (g + 1), [g], [g + 1], [], reuse="pair_hidden%d" % g)
+                add_and_store(g)
+                product(g + 1, 0)
+                product(g + 1, 1)
+        stage("stage3", [2], [3, 4], [3, 4], reuse="pair_hidden2")
+        add_and_store(2)
+        product(3, 0)
+        product(3, 1)
+        product(4, 0)
+        add_and_store(3)
+        product(4, 1)
+        add_and_store(4)

@@ -65,18 +65,19 @@ def tile_moe_loc_mlp_silu_kernel(
         w1_raw = [sb("w1_raw%d" % g, [P, 2 * 2 * H], U8) for g in range(PAIRS)]
         w1_stack = [sb("w1_stack%d" % g, [P, H], U8) for g in range(2)]
         w1_perm = {}
-        w1_plane = {e: sb("w1_plane%d" % e, [P, H], U8) for e in range(E) if e % STACK}
+        moved = [e for e in range(E) if e % STACK]
+        w1_moved = sb("w1_moved", [P, len(moved) * H], U8)
+        w1_plane = {e: w1_moved[:, k * H : (k + 1) * H] for k, e in enumerate(moved)}
         w2_all = sb("w2_all", [P, E * 2 * N], U8)
         w2_plane = sb("w2_plane", [P, E * N], U8)
         gate_t = [sb("gate%d" % r, [P, T], F32) for r in range(2)]
         y = [sb("y%d" % b, [P, S], F32) for b in range(ROW_BLOCKS)]
 
+        nc.vector.memset(w1_stack[0][:].bitcast(I32), 0)
         nc.vector.memset(other_words[:, Q:], 0)
-        for stack in w1_stack:
-            nc.gpsimd.memset(stack[:].bitcast(I32), 0)
-        for e in sorted(w1_plane):
-            nc.gpsimd.memset(w1_plane[e][:].bitcast(I32), 0)
         nc.vector.memset(w2_plane[:].bitcast(I32), 0)
+        nc.vector.memset(w1_moved[:].bitcast(I32), 0)
+        nc.vector.memset(w1_stack[1][:].bitcast(I32), 0)
         nc.vector.memset(other_plane[:].bitcast(I32), 0)
 
         xo_halves = xo.rearrange("(p u j) t -> p u (j t)", u=2, j=2)
@@ -111,8 +112,8 @@ def tile_moe_loc_mlp_silu_kernel(
 
         def permute_w1_stack(g, reuse):
             first = STACK * g
-            w1_plane[first] = sb("w1_plane%d" % first, [P, H], U8, reuse=reuse)
-            permute_columns(w1_plane[first][:], w1_stack[g][:], LINE)
+            w1_plane[first] = sb("w1_plane%d" % first, [P, H], U8, reuse=reuse)[:]
+            permute_columns(w1_plane[first], w1_stack[g][:], LINE)
             for e in range(first + 1, min(first + STACK, E)):
                 place = PACK * (e - first)
                 nc.sync.dma_start(

@@ -26,12 +26,12 @@ PER_COLUMN = 16
 LINE = 16
 ROW_BLOCKS = N // P
 FIRST_BANKS, SECOND_BANKS = 5, 3
-STACK = 4
-MOVED_ROWS = 112
+MOVED_ROWS = 104
 WINDOW = 2 * Q
 
-PIECES = ((0, 0, 384), (0, 384, 768), (1, 0, 320), (1, 320, 640), (1, 640, 768))
+PIECES = ((0, 0, 768), (1, 0, 320), (1, 320, 640), (1, 640, 768))
 PAIRS = E // 2
+DEFERRED = E - 2
 
 
 def tile_moe_loc_mlp_silu_kernel(
@@ -63,21 +63,19 @@ def tile_moe_loc_mlp_silu_kernel(
         xo_raw = [sb("xo_raw%d" % u, [P, 2 * T], F32) for u in range(2)]
         xo_pairs = [sb("xo_pairs%d" % u, [P, 2 * T], BF16) for u in range(2)]
         w1_raw = [sb("w1_raw%d" % g, [P, 2 * 2 * H], U8) for g in range(PAIRS)]
-        w1_stack = [sb("w1_stack%d" % g, [P, H], U8) for g in range(2)]
+        w1_stack = sb("w1_stack", [P, H], U8)
         w1_perm = {}
-        moved = [e for e in range(E) if e % STACK]
-        w1_moved = sb("w1_moved", [P, len(moved) * H], U8)
-        w1_plane = {e: w1_moved[:, k * H : (k + 1) * H] for k, e in enumerate(moved)}
+        w1_moved = sb("w1_moved", [P, (E - 1) * H], U8)
+        w1_plane = {e: w1_moved[:, (e - 1) * H : e * H] for e in range(1, E)}
         w2_all = sb("w2_all", [P, E * 2 * N], U8)
         w2_plane = sb("w2_plane", [P, E * N], U8)
         gate_t = [sb("gate%d" % r, [P, T], F32) for r in range(2)]
         y = [sb("y%d" % b, [P, S], F32) for b in range(ROW_BLOCKS)]
 
-        nc.vector.memset(w1_stack[0][:].bitcast(I32), 0)
+        nc.vector.memset(w1_stack[:].bitcast(I32), 0)
         nc.vector.memset(other_words[:, Q:], 0)
         nc.vector.memset(w2_plane[:].bitcast(I32), 0)
         nc.vector.memset(w1_moved[:].bitcast(I32), 0)
-        nc.vector.memset(w1_stack[1][:].bitcast(I32), 0)
         nc.vector.memset(other_plane[:].bitcast(I32), 0)
 
         xo_halves = xo.rearrange("(p u j) t -> p u (j t)", u=2, j=2)
@@ -91,12 +89,11 @@ def tile_moe_loc_mlp_silu_kernel(
             for r in range(PACK):
                 nc.sync.dma_start(dst[r:P:QUADRANT], rows[:, r:SCALE_ROWS:PACK, :].rearrange("m q c -> q m c"))
 
-        def load_w1_stack(g):
-            lo, hi = STACK * g, min(STACK * (g + 1), E)
+        def load_w1_stack():
             for q in range(P // QUADRANT):
                 nc.sync.dma_start(
-                    w1_stack[g][QUADRANT * q : QUADRANT * q + PACK * (hi - lo), :].bitcast(I32),
-                    w1_scales.bitcast(I32)[lo:hi, 0, PACK * q : PACK * (q + 1), :],
+                    w1_stack[QUADRANT * q : QUADRANT * q + PACK * E, :].bitcast(I32),
+                    w1_scales.bitcast(I32)[:, 0, PACK * q : PACK * (q + 1), :],
                 )
 
         def load_w1_words(g):
@@ -104,28 +101,24 @@ def tile_moe_loc_mlp_silu_kernel(
                 w1_raw[g][:].bitcast(I32).rearrange("p (e c) -> p e c", e=2), w1_rows[:, 2 * g : 2 * g + 2, :]
             )
 
-        def permute_columns(dst, src, run):
+        def permute_columns(dst, src, run, experts=1):
             nc.vector.tensor_copy(
-                dst.rearrange("p (t c i) -> p c t i", t=PACK, i=run),
-                src.rearrange("p (c i t) -> p c t i", t=PACK, i=run),
+                dst.rearrange("p (e t c i) -> p e c t i", e=experts, t=PACK, i=run),
+                src.rearrange("p (e c i t) -> p e c t i", e=experts, t=PACK, i=run),
             )
 
-        def permute_w1_stack(g, reuse):
-            first = STACK * g
-            w1_plane[first] = sb("w1_plane%d" % first, [P, H], U8, reuse=reuse)[:]
-            permute_columns(w1_plane[first], w1_stack[g][:], LINE)
-            for e in range(first + 1, min(first + STACK, E)):
-                place = PACK * (e - first)
-                nc.sync.dma_start(
-                    w1_plane[e][0:MOVED_ROWS, :].bitcast(I32),
-                    w1_plane[first][place : place + MOVED_ROWS, :].bitcast(I32),
-                )
+        def move_plane(e):
+            nc.sync.dma_start(
+                w1_plane[e][0:MOVED_ROWS, :].bitcast(I32),
+                w1_plane[0][PACK * e : PACK * e + MOVED_ROWS, :].bitcast(I32),
+            )
 
-        def permute_w1_words(e, reuse):
-            pair, k = divmod(e, 2)
-            w1_perm[e] = sb("w1_perm%d" % e, [P, 2 * H], U8, reuse=reuse)
-            raw = w1_raw[pair][:, k * 2 * H : (k + 1) * 2 * H]
-            permute_columns(w1_perm[e][:].bitcast(U16), raw.bitcast(U16), LINE // 2)
+        def permute_w1_words(lo, hi, reuse):
+            perm = sb("w1_perm%d" % lo, [P, (hi - lo) * 2 * H], U8, reuse=reuse)
+            raw = w1_raw[lo // 2][:, (lo % 2) * 2 * H : (lo % 2 + hi - lo) * 2 * H]
+            permute_columns(perm[:].bitcast(U16), raw.bitcast(U16), LINE // 2, hi - lo)
+            for e in range(lo, hi):
+                w1_perm[e] = perm[:, (e - lo) * 2 * H : (e - lo + 1) * 2 * H]
 
         def list_columns(lo, hi):
             return slice(lo // PER_COLUMN, hi // PER_COLUMN)
@@ -173,19 +166,22 @@ def tile_moe_loc_mlp_silu_kernel(
                     SILU,
                 )
 
+        def row_block(acc, e, b, codes, plane):
+            col = e * N + b * P
+            nc.tensor.matmul_mx(
+                out=acc,
+                lhsT=w2_all[:, 2 * col : 2 * (col + P)].bitcast(FP4X4),
+                lhsT_scale=w2_plane[:, col : col + P],
+                rhs=codes.bitcast(FP8X4),
+                rhs_scale=plane,
+                start=True,
+                stop=True,
+            )
+
         def second_layer(e, codes, plane):
-            acc = bank("second", SECOND_BANKS)
+            acc = bank("first", FIRST_BANKS)
             for b in range(ROW_BLOCKS):
-                col = e * N + b * P
-                nc.tensor.matmul_mx(
-                    out=acc[:, b * C : (b + 1) * C],
-                    lhsT=w2_all[:, 2 * col : 2 * (col + P)].bitcast(FP4X4),
-                    lhsT_scale=w2_plane[:, col : col + P],
-                    rhs=codes.bitcast(FP8X4),
-                    rhs_scale=plane,
-                    start=True,
-                    stop=True,
-                )
+                row_block(acc[:, b * C : (b + 1) * C], e, b, codes, plane)
             return acc
 
         nc.sync.dma_start(offs2_t[:], offs2)
@@ -193,7 +189,7 @@ def tile_moe_loc_mlp_silu_kernel(
         for u in range(2):
             nc.scalar.dma_start(xo_raw[u][:], xo_halves[:, u, :])
         nc.sync.dma_start(offs_t[:], offs)
-        load_w1_stack(0)
+        load_w1_stack()
         load_w1_words(0)
 
         for u in range(2):
@@ -211,15 +207,18 @@ def tile_moe_loc_mlp_silu_kernel(
             nc.vector.tensor_copy(picked_words[g][:], other_words[:].bitcast(U32).indirect(entries))
 
         woven = {0: weave(0, gather_own(0))}
-        permute_w1_words(0, reuse="xo_raw1")
         woven[1] = weave(1, gather_own(1))
-        permute_w1_stack(0, reuse="xo_raw0")
-        permute_w1_words(1, reuse="woven0")
+        permute_w1_words(0, 1, reuse="xo_raw1")
+        w1_plane[0] = sb("w1_plane0", [P, H], U8, reuse="xo_raw0")[:]
+        permute_columns(w1_plane[0], w1_stack[:], LINE)
+        for e in range(1, E):
+            move_plane(e)
+        permute_w1_words(1, 2, reuse="woven0")
         load_plane(w2_plane[:], w2_scales.rearrange("e s b n -> (e s) b n"), N)
-        load_w1_stack(1)
         load_w1_words(2)
 
         hidden = {}
+        h_codes = {}
         for e in range(E + 1):
             if e < E:
                 x_codes, x_plane = quantize("x%d" % e, woven[e][:].bitcast(BF16), C)
@@ -228,16 +227,20 @@ def tile_moe_loc_mlp_silu_kernel(
             if e < E:
                 hidden[e] = sb("hidden%d" % e, [P, PACK * C], BF16)
                 first_layer(hidden[e][:], e, x_codes, x_plane)
-            if e >= 1:
-                acc = second_layer(e - 1, *quantize("h%d" % (e - 1), hidden[e - 1][:], C))
-                for b in range(ROW_BLOCKS):
-                    nc.scalar.copy(y[b][:, (e - 1) * C : e * C], acc[:, b * C : (b + 1) * C])
-            if 2 <= e + 1 < E:
-                permute_w1_words(e + 1, reuse="x%d_plane" % (e - 1))
             if e + 2 < E:
                 woven[e + 2] = weave(e + 2, halves)
+            if e >= 1:
+                h_codes[e - 1] = quantize("h%d" % (e - 1), hidden[e - 1][:], C)
+            for done in {4: (), 5: (3, 4)}.get(e, (e - 1,) if e >= 1 else ()):
+                acc = bank("second", SECOND_BANKS)
+                blocks = range(1 if done >= DEFERRED else ROW_BLOCKS)
+                for b in blocks:
+                    row_block(acc[:, b * C : (b + 1) * C], done, b, *h_codes[done])
+                for b in blocks:
+                    nc.scalar.copy(y[b][:, done * C : (done + 1) * C], acc[:, b * C : (b + 1) * C])
+            if e in (1, 3):
+                permute_w1_words(e + 1, e + 3, reuse="x%d_plane" % (e - 1))
             if e == 1:
-                permute_w1_stack(1, reuse="woven1")
                 load_plane(other_plane[:, :Q], x_scales, Q)
                 nc.sync.dma_start(pos_t[0][:], pos1)
                 nc.sync.dma_start(pos_t[1][:], pos2)
@@ -247,15 +250,20 @@ def tile_moe_loc_mlp_silu_kernel(
         picked_plane = {}
         last = E - 1
         for lo, hi, reuse in (
-            (0, 1, "hidden2"),
-            (1, 2, "halves%d" % last),
-            (2, 4, "hidden%d" % (last - 1)),
+            (0, 1, "halves%d" % (last - 1)),
+            (1, 3, "halves%d" % last),
+            (3, 4, "hidden%d" % (last - 1)),
             (4, E, "hidden%d" % last),
         ):
             part = sb("picked_plane%d" % lo, [P, (hi - lo) * C], U8, reuse=reuse)
             nc.vector.tensor_copy(part[:], other_plane[:].indirect(offs2_t[:, list_columns(lo * C, hi * C)]))
             for e in range(lo, hi):
                 picked_plane[e] = part[:, (e - lo) * C : (e - lo + 1) * C]
+
+        acc = bank("second", SECOND_BANKS)
+        for e in range(DEFERRED, E):
+            row_block(acc[:, (e - DEFERRED) * C : (e - DEFERRED + 1) * C], e, 1, *h_codes[e])
+        nc.scalar.copy(y[1][:, DEFERRED * C :], acc[:])
 
         pair_hidden = [sb("pair_hidden%d" % g, [P, 2 * PACK * C], BF16) for g in range(PAIRS)]
 
@@ -272,8 +280,13 @@ def tile_moe_loc_mlp_silu_kernel(
         start_pair(0)
         start_pair(1)
 
+        pair_codes = {}
+
+        def quantize_pair(g):
+            pair_codes[g] = quantize("pair%d" % g, pair_hidden[g][:], 2 * C)
+
         def finish_pair(g):
-            codes, plane = quantize("pair%d" % g, pair_hidden[g][:], 2 * C)
+            codes, plane = pair_codes[g]
             for k in range(2):
                 e = 2 * g + k
                 acc = second_layer(e, codes[:, k * C : (k + 1) * C], plane[:, k * C : (k + 1) * C])
@@ -313,23 +326,23 @@ def tile_moe_loc_mlp_silu_kernel(
             nc.vector.tensor_tensor(sums[i], products[i][:, :w], products[i][:, w:], ADD)
             nc.sync.dma_start(out_rows[:, b, lo:hi], sums[i])
 
-        stage("stage0", [], [0], [])
+        start_pair(2)
+        stage("stage0", [0], [0, 1], [])
         product(0, 0)
         product(0, 1)
-        for g in range(PAIRS):
-            finish_pair(g)
-            if g == 0:
-                start_pair(2)
-            if g < PAIRS - 1:
-                stage("stage%d" % (g + 1), [g], [g + 1], [], reuse="pair_hidden%d" % g)
-                add_and_store(g)
-                product(g + 1, 0)
-                product(g + 1, 1)
-        stage("stage3", [2], [3, 4], [3, 4], reuse="pair_hidden2")
+        product(1, 0)
+        add_and_store(0)
+        quantize_pair(0)
+        finish_pair(0)
+        product(1, 1)
+        quantize_pair(1)
+        quantize_pair(2)
+        stage("stage1", [1], [2, 3], [2, 3], reuse="pair_hidden2")
+        add_and_store(1)
+        finish_pair(1)
+        finish_pair(2)
+        for r in range(2):
+            product(2, r)
+            product(3, r)
         add_and_store(2)
-        product(3, 0)
-        product(3, 1)
-        product(4, 0)
         add_and_store(3)
-        product(4, 1)
-        add_and_store(4)

@@ -26,12 +26,14 @@ PER_COLUMN = 16
 LINE = 16
 ROW_BLOCKS = N // P
 FIRST_BANKS, SECOND_BANKS = 5, 3
-MOVED_ROWS = 104
+MOVED_ROWS = 3 * QUADRANT + PACK
 WINDOW = 2 * Q
 
 PIECES = ((0, 0, 768), (1, 0, 320), (1, 320, 640), (1, 640, 768))
 PAIRS = E // 2
 DEFERRED = E - 2
+
+FINISHED = {1: (0,), 2: (1,), 3: (2,), 5: (3, 4), 6: (5,)}
 
 
 def tile_moe_loc_mlp_silu_kernel(
@@ -231,7 +233,7 @@ def tile_moe_loc_mlp_silu_kernel(
                 woven[e + 2] = weave(e + 2, halves)
             if e >= 1:
                 h_codes[e - 1] = quantize("h%d" % (e - 1), hidden[e - 1][:], C)
-            for done in {4: (), 5: (3, 4)}.get(e, (e - 1,) if e >= 1 else ()):
+            for done in FINISHED.get(e, ()):
                 acc = bank("second", SECOND_BANKS)
                 blocks = range(1 if done >= DEFERRED else ROW_BLOCKS)
                 for b in blocks:
@@ -266,19 +268,14 @@ def tile_moe_loc_mlp_silu_kernel(
         nc.scalar.copy(y[1][:, DEFERRED * C :], acc[:])
 
         pair_hidden = [sb("pair_hidden%d" % g, [P, 2 * PACK * C], BF16) for g in range(PAIRS)]
-
-        def start_pair(g):
-            for e in (2 * g, 2 * g + 1):
-                half, k = divmod(e, E // 2)
-                first_layer(
-                    pair_hidden[g][:, (e % 2) * PACK * C : (e % 2 + 1) * PACK * C],
-                    e,
-                    picked_words[half][:, k * C : (k + 1) * C],
-                    picked_plane[e],
-                )
-
-        start_pair(0)
-        start_pair(1)
+        for e in range(E):
+            half, k = divmod(e, E // 2)
+            first_layer(
+                pair_hidden[e // 2][:, (e % 2) * PACK * C : (e % 2 + 1) * PACK * C],
+                e,
+                picked_words[half][:, k * C : (k + 1) * C],
+                picked_plane[e],
+            )
 
         pair_codes = {}
 
@@ -290,7 +287,7 @@ def tile_moe_loc_mlp_silu_kernel(
             for k in range(2):
                 e = 2 * g + k
                 acc = second_layer(e, codes[:, k * C : (k + 1) * C], plane[:, k * C : (k + 1) * C])
-                z = sb("z%d" % e, [P, ROW_BLOCKS * C], F32, reuse="")
+                z = sb("z%d" % e, [P, ROW_BLOCKS * C], F32)
                 nc.scalar.copy(z[:], acc[:])
                 nc.sync.dma_start(
                     out_rows[:, :, T + e * C : T + (e + 1) * C], z[:].rearrange("p (b c) -> p b c", b=ROW_BLOCKS)
@@ -300,15 +297,15 @@ def tile_moe_loc_mlp_silu_kernel(
         products = {}
         sums = {}
 
-        def stage(name, done, todo, last_sums, reuse=""):
-            total = sum(widths[i] for i in done + last_sums) + 2 * sum(widths[i] for i in todo)
-            space_of = sb(name, [P, total], F32, reuse=reuse)
+        def stage(name, summed, multiplied, reuse=""):
+            total = sum(widths[i] for i in summed) + 2 * sum(widths[i] for i in multiplied)
+            room = sb(name, [P, total], F32, reuse=reuse)
             at = 0
-            for i in done + last_sums:
-                sums[i] = space_of[:, at : at + widths[i]]
+            for i in summed:
+                sums[i] = room[:, at : at + widths[i]]
                 at = at + widths[i]
-            for i in todo:
-                products[i] = space_of[:, at : at + 2 * widths[i]]
+            for i in multiplied:
+                products[i] = room[:, at : at + 2 * widths[i]]
                 at = at + 2 * widths[i]
 
         def product(i, r):
@@ -326,8 +323,7 @@ def tile_moe_loc_mlp_silu_kernel(
             nc.vector.tensor_tensor(sums[i], products[i][:, :w], products[i][:, w:], ADD)
             nc.sync.dma_start(out_rows[:, b, lo:hi], sums[i])
 
-        start_pair(2)
-        stage("stage0", [0], [0, 1], [])
+        stage("stage0", [0], [0, 1])
         product(0, 0)
         product(0, 1)
         product(1, 0)
@@ -337,7 +333,7 @@ def tile_moe_loc_mlp_silu_kernel(
         product(1, 1)
         quantize_pair(1)
         quantize_pair(2)
-        stage("stage1", [1], [2, 3], [2, 3], reuse="pair_hidden2")
+        stage("stage1", [1, 2, 3], [2, 3], reuse="pair_hidden%d" % (PAIRS - 1))
         add_and_store(1)
         finish_pair(1)
         finish_pair(2)

@@ -103,8 +103,8 @@ def tile_moe_loc_mlp_silu_kernel(
                 w1_raw[g][:].bitcast(I32).rearrange("p (e c) -> p e c", e=2), w1_rows[:, 2 * g : 2 * g + 2, :]
             )
 
-        def permute_columns(dst, src, run, experts=1):
-            nc.vector.tensor_copy(
+        def permute_columns(copy, dst, src, run, experts=1):
+            copy(
                 dst.rearrange("p (e t c i) -> p e c t i", e=experts, t=PACK, i=run),
                 src.rearrange("p (e c i t) -> p e c t i", e=experts, t=PACK, i=run),
             )
@@ -115,10 +115,9 @@ def tile_moe_loc_mlp_silu_kernel(
                 w1_plane[0][PACK * e : PACK * e + MOVED_ROWS, :].bitcast(I32),
             )
 
-        def permute_w1_words(lo, hi, reuse):
-            perm = sb("w1_perm%d" % lo, [P, (hi - lo) * 2 * H], U8, reuse=reuse)
+        def permute_w1_words(copy, lo, hi, perm):
             raw = w1_raw[lo // 2][:, (lo % 2) * 2 * H : (lo % 2 + hi - lo) * 2 * H]
-            permute_columns(perm[:].bitcast(U16), raw.bitcast(U16), LINE // 2, hi - lo)
+            permute_columns(copy, perm.bitcast(U16), raw.bitcast(U16), LINE // 2, hi - lo)
             for e in range(lo, hi):
                 w1_perm[e] = perm[:, (e - lo) * 2 * H : (e - lo + 1) * 2 * H]
 
@@ -190,6 +189,9 @@ def tile_moe_loc_mlp_silu_kernel(
         nc.scalar.dma_start(other_words[:, :Q], x_words[0].rearrange("p t d -> p (t d)").bitcast(I32))
         for u in range(2):
             nc.scalar.dma_start(xo_raw[u][:], xo_halves[:, u, :])
+        warm = sb("warm", [P, 2], F32)
+        nc.gpsimd.memset(warm[:, 0:1], 0.0)
+        nc.scalar.activation(warm[:, 1:2], warm[:, 0:1], SILU)
         nc.sync.dma_start(offs_t[:], offs)
         load_w1_stack()
         load_w1_words(0)
@@ -208,14 +210,16 @@ def tile_moe_loc_mlp_silu_kernel(
             entries = offs2_t[:, list_columns(g * S // 2, (g + 1) * S // 2)]
             nc.vector.tensor_copy(picked_words[g][:], other_words[:].bitcast(U32).indirect(entries))
 
+        after_casts = sb("after_casts", [P, 2 * 2 * H], U8, reuse="xo_raw1")
+        permute_w1_words(nc.scalar.copy, 0, 1, after_casts[:, : 2 * H])
         woven = {0: weave(0, gather_own(0))}
         woven[1] = weave(1, gather_own(1))
-        permute_w1_words(0, 1, reuse="xo_raw1")
         w1_plane[0] = sb("w1_plane0", [P, H], U8, reuse="xo_raw0")[:]
-        permute_columns(w1_plane[0], w1_stack[:], LINE)
+        permute_columns(nc.vector.tensor_copy, w1_plane[0], w1_stack[:], LINE)
         for e in range(1, E):
             move_plane(e)
-        permute_w1_words(1, 2, reuse="woven0")
+        permute_w1_words(nc.vector.tensor_copy, 2, 3, after_casts[:, 2 * H :])
+        permute_w1_words(nc.scalar.copy, 1, 2, sb("w1_perm1", [P, 2 * H], U8, reuse="woven0")[:])
         load_plane(w2_plane[:], w2_scales.rearrange("e s b n -> (e s) b n"), N)
         load_w1_words(2)
 
@@ -240,8 +244,11 @@ def tile_moe_loc_mlp_silu_kernel(
                     row_block(acc[:, b * C : (b + 1) * C], done, b, *h_codes[done])
                 for b in blocks:
                     nc.scalar.copy(y[b][:, done * C : (done + 1) * C], acc[:, b * C : (b + 1) * C])
-            if e in (1, 3):
-                permute_w1_words(e + 1, e + 3, reuse="x%d_plane" % (e - 1))
+            if e == 1:
+                permute_w1_words(nc.vector.tensor_copy, 3, 4, sb("w1_perm3", [P, 2 * H], U8, reuse="x0_plane")[:])
+            if e == 3:
+                perm = sb("w1_perm4", [P, 2 * 2 * H], U8, reuse="x2_plane")
+                permute_w1_words(nc.vector.tensor_copy, 4, E, perm[:])
             if e == 1:
                 load_plane(other_plane[:, :Q], x_scales, Q)
                 nc.sync.dma_start(pos_t[0][:], pos1)

@@ -25,11 +25,11 @@ SCALE_ROWS = 16
 PER_COLUMN = 16
 LINE = 16
 ROW_BLOCKS = N // P
-FIRST_BANKS, SECOND_BANKS = 5, 3
+FIRST_BANKS, SECOND_BANKS = 4, 3
 MOVED_ROWS = 3 * QUADRANT + PACK
 WINDOW = 2 * Q
 
-PIECES = ((0, 0, 768), (1, 0, 320), (1, 320, 640), (1, 640, 768))
+PIECES = ((0, 0, 768), (1, 0, 352), (1, 352, 640), (1, 640, 768))
 PAIRS = E // 2
 DEFERRED = E - 2
 
@@ -179,12 +179,6 @@ def tile_moe_loc_mlp_silu_kernel(
                 stop=True,
             )
 
-        def second_layer(e, codes, plane):
-            acc = bank("first", FIRST_BANKS)
-            for b in range(ROW_BLOCKS):
-                row_block(acc[:, b * C : (b + 1) * C], e, b, codes, plane)
-            return acc
-
         nc.sync.dma_start(offs2_t[:], offs2)
         nc.scalar.dma_start(other_words[:, :Q], x_words[0].rearrange("p t d -> p (t d)").bitcast(I32))
         for u in range(2):
@@ -275,7 +269,8 @@ def tile_moe_loc_mlp_silu_kernel(
         nc.scalar.copy(y[1][:, DEFERRED * C :], acc[:])
 
         pair_hidden = [sb("pair_hidden%d" % g, [P, 2 * PACK * C], BF16) for g in range(PAIRS)]
-        for e in range(E):
+
+        def other_first_layer(e):
             half, k = divmod(e, E // 2)
             first_layer(
                 pair_hidden[e // 2][:, (e % 2) * PACK * C : (e % 2 + 1) * PACK * C],
@@ -284,6 +279,9 @@ def tile_moe_loc_mlp_silu_kernel(
                 picked_plane[e],
             )
 
+        for e in range(E - 1):
+            other_first_layer(e)
+
         pair_codes = {}
 
         def quantize_pair(g):
@@ -291,14 +289,14 @@ def tile_moe_loc_mlp_silu_kernel(
 
         def finish_pair(g):
             codes, plane = pair_codes[g]
-            for k in range(2):
-                e = 2 * g + k
-                acc = second_layer(e, codes[:, k * C : (k + 1) * C], plane[:, k * C : (k + 1) * C])
-                z = sb("z%d" % e, [P, ROW_BLOCKS * C], F32)
+            for b in range(ROW_BLOCKS):
+                acc = bank("first", FIRST_BANKS)
+                for k in range(2):
+                    cols = slice(k * C, (k + 1) * C)
+                    row_block(acc[:, cols], 2 * g + k, b, codes[:, cols], plane[:, cols])
+                z = sb("z%d%d" % (g, b), [P, 2 * C], F32)
                 nc.scalar.copy(z[:], acc[:])
-                nc.sync.dma_start(
-                    out_rows[:, :, T + e * C : T + (e + 1) * C], z[:].rearrange("p (b c) -> p b c", b=ROW_BLOCKS)
-                )
+                nc.sync.dma_start(out_rows[:, b, T + 2 * g * C : T + 2 * (g + 1) * C], z[:])
 
         widths = [hi - lo for b, lo, hi in PIECES]
         products = {}
@@ -330,18 +328,20 @@ def tile_moe_loc_mlp_silu_kernel(
             nc.vector.tensor_tensor(sums[i], products[i][:, :w], products[i][:, w:], ADD)
             nc.sync.dma_start(out_rows[:, b, lo:hi], sums[i])
 
-        stage("stage0", [0], [0, 1])
+        stage("stage0", [], [0])
         product(0, 0)
         product(0, 1)
+        quantize_pair(0)
+        stage("stage01", [0, 1], [1], reuse="picked_plane3")
         product(1, 0)
         add_and_store(0)
-        quantize_pair(0)
         finish_pair(0)
+        other_first_layer(E - 1)
         product(1, 1)
         quantize_pair(1)
-        quantize_pair(2)
-        stage("stage1", [1, 2, 3], [2, 3], reuse="pair_hidden%d" % (PAIRS - 1))
         add_and_store(1)
+        quantize_pair(2)
+        stage("stage1", [2, 3], [2, 3], reuse="pair_hidden%d" % (PAIRS - 1))
         finish_pair(1)
         finish_pair(2)
         for r in range(2):

@@ -29,8 +29,9 @@ FIRST_BANKS, SECOND_BANKS = 4, 3
 MOVED_ROWS = 3 * QUADRANT + PACK
 WINDOW = 2 * Q
 
-PIECES = ((0, 0, 768), (1, 0, 352), (1, 352, 640), (1, 640, 768))
+PIECES = ((0, 0, 768), (1, 0, 288), (1, 288, 640), (1, 640, 768))
 PAIRS = E // 2
+VECTOR_CAST = 160
 DEFERRED = E - 2
 
 FINISHED = {1: (0,), 2: (1,), 3: (2,), 5: (3, 4), 6: (5,)}
@@ -46,9 +47,9 @@ def tile_moe_loc_mlp_silu_kernel(
 
         turns = {"first": 0, "second": 0}
 
-        def bank(layer, count):
-            tag = "%s%d" % (layer, turns[layer] % count)
-            turns[layer] = turns[layer] + 1
+        def bank(layer, count, skip=0):
+            tag = "%s%d" % (layer, (turns[layer] + skip) % count)
+            turns[layer] = turns[layer] + skip + 1
             return psum.tile([P, PACK * P], F32, name=tag, tag=tag)
 
         space = {}
@@ -190,11 +191,15 @@ def tile_moe_loc_mlp_silu_kernel(
         load_w1_stack()
         load_w1_words(0)
 
-        for u in range(2):
-            nc.scalar.copy(
-                xo_pairs[u][:].rearrange("p (t j) -> p t j", j=2),
-                xo_raw[u][:].rearrange("p (j t) -> p t j", j=2),
+        def cast(copy, u, lo, hi):
+            copy(
+                xo_pairs[u][:].rearrange("p (t j) -> p t j", j=2)[:, lo:hi, :],
+                xo_raw[u][:].rearrange("p (j t) -> p t j", j=2)[:, lo:hi, :],
             )
+
+        cast(nc.scalar.copy, 0, 0, T)
+        cast(nc.vector.tensor_copy, 1, 0, VECTOR_CAST)
+        cast(nc.scalar.copy, 1, VECTOR_CAST, T)
 
         load_w1_words(1)
         nc.sync.dma_start(w2_all[:].bitcast(I32).rearrange("p (e c) -> p e c", e=E), w2_rows)
@@ -254,8 +259,7 @@ def tile_moe_loc_mlp_silu_kernel(
         last = E - 1
         for lo, hi, reuse in (
             (0, 1, "halves%d" % (last - 1)),
-            (1, 3, "halves%d" % last),
-            (3, 4, "hidden%d" % (last - 1)),
+            (1, 4, "halves%d" % last),
             (4, E, "hidden%d" % last),
         ):
             part = sb("picked_plane%d" % lo, [P, (hi - lo) * C], U8, reuse=reuse)
@@ -287,10 +291,10 @@ def tile_moe_loc_mlp_silu_kernel(
         def quantize_pair(g):
             pair_codes[g] = quantize("pair%d" % g, pair_hidden[g][:], 2 * C)
 
-        def finish_pair(g):
+        def finish_pair(g, skip=0):
             codes, plane = pair_codes[g]
             for b in range(ROW_BLOCKS):
-                acc = bank("first", FIRST_BANKS)
+                acc = bank("first", FIRST_BANKS, skip=skip if b == 0 else 0)
                 for k in range(2):
                     cols = slice(k * C, (k + 1) * C)
                     row_block(acc[:, cols], 2 * g + k, b, codes[:, cols], plane[:, cols])
@@ -299,24 +303,19 @@ def tile_moe_loc_mlp_silu_kernel(
                 nc.sync.dma_start(out_rows[:, b, T + 2 * g * C : T + 2 * (g + 1) * C], z[:])
 
         widths = [hi - lo for b, lo, hi in PIECES]
-        products = {}
-        sums = {}
+        room = {}
 
-        def stage(name, summed, multiplied, reuse=""):
-            total = sum(widths[i] for i in summed) + 2 * sum(widths[i] for i in multiplied)
-            room = sb(name, [P, total], F32, reuse=reuse)
+        def stage(name, parts, reuse=""):
+            whole = sb(name, [P, sum(widths[i] for i, k in parts)], F32, reuse=reuse)
             at = 0
-            for i in summed:
-                sums[i] = room[:, at : at + widths[i]]
+            for i, k in parts:
+                room[i, k] = whole[:, at : at + widths[i]]
                 at = at + widths[i]
-            for i in multiplied:
-                products[i] = room[:, at : at + 2 * widths[i]]
-                at = at + 2 * widths[i]
 
         def product(i, r):
             b, lo, hi = PIECES[i]
             nc.vector.tensor_tensor(
-                products[i][:, r * widths[i] : (r + 1) * widths[i]],
+                room[i, r],
                 y[b][:].indirect(pos_t[r][:, list_columns(lo, hi)]),
                 gate_t[r][:, lo:hi],
                 MULT,
@@ -324,15 +323,14 @@ def tile_moe_loc_mlp_silu_kernel(
 
         def add_and_store(i):
             b, lo, hi = PIECES[i]
-            w = widths[i]
-            nc.vector.tensor_tensor(sums[i], products[i][:, :w], products[i][:, w:], ADD)
-            nc.sync.dma_start(out_rows[:, b, lo:hi], sums[i])
+            nc.vector.tensor_tensor(room[i, 2], room[i, 0], room[i, 1], ADD)
+            nc.sync.dma_start(out_rows[:, b, lo:hi], room[i, 2])
 
-        stage("stage0", [], [0])
+        stage("stage0", [(0, 0), (0, 1)])
         product(0, 0)
         product(0, 1)
         quantize_pair(0)
-        stage("stage01", [0, 1], [1], reuse="picked_plane3")
+        stage("stage1", [(0, 2), (1, 0), (1, 1), (1, 2), (3, 0)], reuse="picked_plane1")
         product(1, 0)
         add_and_store(0)
         finish_pair(0)
@@ -340,12 +338,13 @@ def tile_moe_loc_mlp_silu_kernel(
         product(1, 1)
         quantize_pair(1)
         add_and_store(1)
+        product(3, 0)
         quantize_pair(2)
-        stage("stage1", [2, 3], [2, 3], reuse="pair_hidden%d" % (PAIRS - 1))
-        finish_pair(1)
+        finish_pair(1, skip=FIRST_BANKS - 2)
+        stage("stage2", [(2, 0), (2, 1), (2, 2), (3, 1), (3, 2)], reuse="pair1_codes")
         finish_pair(2)
-        for r in range(2):
-            product(2, r)
-            product(3, r)
+        product(2, 0)
+        product(2, 1)
+        product(3, 1)
         add_and_store(2)
         add_and_store(3)

@@ -29,7 +29,7 @@ FIRST_BANKS, SECOND_BANKS = 4, 3
 MOVED_ROWS = 3 * QUADRANT + PACK
 WINDOW = 2 * Q
 
-PIECES = ((0, 0, 768), (1, 0, 288), (1, 288, 640), (1, 640, 768))
+PIECES = ((0, 0, 768), (1, 0, 384), (1, 384, 640), (1, 640, 768))
 PAIRS = E // 2
 VECTOR_CAST = 160
 DEFERRED = E - 2
@@ -148,8 +148,8 @@ def tile_moe_loc_mlp_silu_kernel(
             )
             return woven
 
-        def first_layer(hidden, e, codes, plane):
-            for block in range(C // P):
+        def first_layer(hidden, e, codes, plane, blocks=range(C // P)):
+            for block in blocks:
                 cols = slice(block * P, (block + 1) * P)
                 acc = bank("first", FIRST_BANKS)
                 for t in range(PACK):
@@ -272,35 +272,48 @@ def tile_moe_loc_mlp_silu_kernel(
             row_block(acc[:, (e - DEFERRED) * C : (e - DEFERRED + 1) * C], e, 1, *h_codes[e])
         nc.scalar.copy(y[1][:, DEFERRED * C :], acc[:])
 
-        pair_hidden = [sb("pair_hidden%d" % g, [P, 2 * PACK * C], BF16) for g in range(PAIRS)]
+        groups = ((0, 2), (2, 4), (4, 5), (5, 6))
+        group_hidden = [sb("other_hidden%d" % lo, [P, (hi - lo) * PACK * C], BF16) for lo, hi in groups]
+        other_hidden = {}
+        for g, (lo, hi) in enumerate(groups):
+            for e in range(lo, hi):
+                other_hidden[e] = group_hidden[g][:, (e - lo) * PACK * C : (e - lo + 1) * PACK * C]
 
-        def other_first_layer(e):
+        def other_block(e, block):
             half, k = divmod(e, E // 2)
-            first_layer(
-                pair_hidden[e // 2][:, (e % 2) * PACK * C : (e % 2 + 1) * PACK * C],
-                e,
-                picked_words[half][:, k * C : (k + 1) * C],
-                picked_plane[e],
+            first_layer(other_hidden[e], e, picked_words[half][:, k * C : (k + 1) * C], picked_plane[e], [block])
+
+        group_codes = {}
+
+        def quantize_group(g):
+            lo, hi = groups[g]
+            group_codes[g] = quantize("group%d" % g, group_hidden[g][:], (hi - lo) * C)
+
+        def pair_rows(g, b):
+            codes, plane = group_codes[g]
+            acc = bank("first", FIRST_BANKS)
+            for k in range(2):
+                cols = slice(k * C, (k + 1) * C)
+                row_block(acc[:, cols], 2 * g + k, b, codes[:, cols], plane[:, cols])
+            z = sb("z%d%d" % (g, b), [P, 2 * C], F32)
+            nc.scalar.copy(z[:], acc[:])
+            nc.sync.dma_start(out_rows[:, b, T + 2 * g * C : T + 2 * (g + 1) * C], z[:])
+
+        def single_rows(g, skip=0):
+            e = groups[g][0]
+            acc = bank("first", FIRST_BANKS, skip)
+            for b in range(ROW_BLOCKS):
+                row_block(acc[:, b * C : (b + 1) * C], e, b, *group_codes[g])
+            z = sb("z%d" % e, [P, ROW_BLOCKS * C], F32)
+            nc.scalar.copy(z[:], acc[:])
+            nc.sync.dma_start(
+                out_rows[:, :, T + e * C : T + (e + 1) * C], z[:].rearrange("p (b c) -> p b c", b=ROW_BLOCKS)
             )
 
-        for e in range(E - 1):
-            other_first_layer(e)
-
-        pair_codes = {}
-
-        def quantize_pair(g):
-            pair_codes[g] = quantize("pair%d" % g, pair_hidden[g][:], 2 * C)
-
-        def finish_pair(g, skip=0):
-            codes, plane = pair_codes[g]
-            for b in range(ROW_BLOCKS):
-                acc = bank("first", FIRST_BANKS, skip=skip if b == 0 else 0)
-                for k in range(2):
-                    cols = slice(k * C, (k + 1) * C)
-                    row_block(acc[:, cols], 2 * g + k, b, codes[:, cols], plane[:, cols])
-                z = sb("z%d%d" % (g, b), [P, 2 * C], F32)
-                nc.scalar.copy(z[:], acc[:])
-                nc.sync.dma_start(out_rows[:, b, T + 2 * g * C : T + 2 * (g + 1) * C], z[:])
+        for e in range(4):
+            for block in range(C // P):
+                other_block(e, block)
+        other_block(4, 0)
 
         widths = [hi - lo for b, lo, hi in PIECES]
         room = {}
@@ -329,20 +342,28 @@ def tile_moe_loc_mlp_silu_kernel(
         stage("stage0", [(0, 0), (0, 1)])
         product(0, 0)
         product(0, 1)
-        quantize_pair(0)
-        stage("stage1", [(0, 2), (1, 0), (1, 1), (1, 2), (3, 0)], reuse="picked_plane1")
+        quantize_group(0)
+        stage("stage1", [(0, 2), (1, 0)], reuse="picked_plane1")
         product(1, 0)
         add_and_store(0)
-        finish_pair(0)
-        other_first_layer(E - 1)
+        pair_rows(0, 0)
+        other_block(4, 1)
+        pair_rows(0, 1)
+        other_block(5, 0)
+        quantize_group(1)
+        stage("stage2", [(1, 1)], reuse="group0_codes")
         product(1, 1)
-        quantize_pair(1)
+        pair_rows(1, 0)
+        other_block(5, 1)
+        quantize_group(2)
+        stage("stage2b", [(1, 2), (3, 0)], reuse="picked_plane4")
         add_and_store(1)
         product(3, 0)
-        quantize_pair(2)
-        finish_pair(1, skip=FIRST_BANKS - 2)
-        stage("stage2", [(2, 0), (2, 1), (2, 2), (3, 1), (3, 2)], reuse="pair1_codes")
-        finish_pair(2)
+        quantize_group(3)
+        pair_rows(1, 1)
+        single_rows(2, skip=FIRST_BANKS - 2)
+        single_rows(3)
+        stage("stage3", [(2, 0), (2, 1), (2, 2), (3, 1), (3, 2)], reuse="group2_codes")
         product(2, 0)
         product(2, 1)
         product(3, 1)

@@ -43,6 +43,7 @@ def tile_moe_loc_mlp_silu_kernel(
     nc = tc.nc
     with ExitStack() as ctx:
         keep = ctx.enter_context(tc.tile_pool(name="keep", bufs=1))
+        shared = ctx.enter_context(tc.tile_pool(name="shared", bufs=1))
         psum = ctx.enter_context(tc.psum_pool(name="psum", bufs=1))
 
         turns = {"first": 0, "second": 0}
@@ -57,6 +58,9 @@ def tile_moe_loc_mlp_silu_kernel(
         def sb(name, shape, dtype, reuse=""):
             space[name] = space[reuse] if reuse else name
             return keep.tile(shape, dtype, name=name, tag=space[name], align_bytes=64)
+
+        def placed(name, shape, dtype, offset):
+            return shared.tile(shape, dtype, name=name, tag=name, offset=offset, align_bytes=64)
 
         offs_t = sb("offs_t", [P, S // PER_COLUMN], U16)
         offs2_t = sb("offs2_t", [P, S // PER_COLUMN], U16)
@@ -132,7 +136,10 @@ def tile_moe_loc_mlp_silu_kernel(
             return codes[:], plane[:]
 
         def gather_own(e):
-            halves = sb("halves%d" % e, [P, 2 * C], U32, reuse="halves%d" % (e - 2) if e >= 2 else "")
+            if e % 2:
+                halves = sb("halves%d" % e, [P, 2 * C], U32, reuse="halves%d" % (e - 2) if e >= 2 else "")
+            else:
+                halves = placed("halves%d" % e, [P, 2 * C], U32, 0 if e else 2 * H)
             for u in range(2):
                 nc.vector.tensor_copy(
                     halves[:, u * C : (u + 1) * C],
@@ -209,18 +216,20 @@ def tile_moe_loc_mlp_silu_kernel(
             entries = offs2_t[:, list_columns(g * S // 2, (g + 1) * S // 2)]
             nc.vector.tensor_copy(picked_words[g][:], other_words[:].bitcast(U32).indirect(entries))
 
-        after_casts = sb("after_casts", [P, 2 * 2 * H], U8, reuse="xo_raw1")
-        permute_w1_words(nc.scalar.copy, 0, 1, after_casts[:, : 2 * H])
+        after_casts = sb("after_casts", [P, 5 * H], U8, reuse="xo_raw1")
+        permute_w1_words(nc.scalar.copy, 0, 2, after_casts[:, : 4 * H])
         woven = {0: weave(0, gather_own(0))}
-        woven[1] = weave(1, gather_own(1))
-        w1_plane[0] = sb("w1_plane0", [P, H], U8, reuse="xo_raw0")[:]
+        w1_plane[0] = after_casts[:, 4 * H :]
         permute_columns(nc.vector.tensor_copy, w1_plane[0], w1_stack[:], LINE)
-        for e in range(1, E):
+        permute_w1_words(nc.scalar.copy, 2, 3, placed("w1_perm2", [P, 2 * H], U8, 4 * H)[:])
+        woven[1] = weave(1, gather_own(1))
+        for e in range(1, 4):
             move_plane(e)
-        permute_w1_words(nc.vector.tensor_copy, 2, 3, after_casts[:, 2 * H :])
-        permute_w1_words(nc.scalar.copy, 1, 2, sb("w1_perm1", [P, 2 * H], U8, reuse="woven0")[:])
         load_plane(w2_plane[:], w2_scales.rearrange("e s b n -> (e s) b n"), N)
+        load_plane(other_plane[:, :Q], x_scales, Q)
         load_w1_words(2)
+        for e in range(4, E):
+            move_plane(e)
 
         hidden = {}
         h_codes = {}
@@ -249,7 +258,6 @@ def tile_moe_loc_mlp_silu_kernel(
                 perm = sb("w1_perm4", [P, 2 * 2 * H], U8, reuse="x2_plane")
                 permute_w1_words(nc.vector.tensor_copy, 4, E, perm[:])
             if e == 1:
-                load_plane(other_plane[:, :Q], x_scales, Q)
                 nc.sync.dma_start(pos_t[0][:], pos1)
                 nc.sync.dma_start(pos_t[1][:], pos2)
                 for r in range(2):
@@ -262,7 +270,10 @@ def tile_moe_loc_mlp_silu_kernel(
             (1, 4, "halves%d" % last),
             (4, E, "hidden%d" % last),
         ):
-            part = sb("picked_plane%d" % lo, [P, (hi - lo) * C], U8, reuse=reuse)
+            if lo:
+                part = sb("picked_plane%d" % lo, [P, (hi - lo) * C], U8, reuse=reuse)
+            else:
+                part = placed("picked_plane0", [P, C], U8, 0)
             nc.vector.tensor_copy(part[:], other_plane[:].indirect(offs2_t[:, list_columns(lo * C, hi * C)]))
             for e in range(lo, hi):
                 picked_plane[e] = part[:, (e - lo) * C : (e - lo + 1) * C]

@@ -126,6 +126,15 @@ def tile_moe_loc_mlp_silu_kernel(
             for e in range(lo, hi):
                 w1_perm[e] = perm[:, (e - lo) * 2 * H : (e - lo + 1) * 2 * H]
 
+        def permute_in_sweeps(dst, src):
+            nc.gpsimd.tensor_copy(dst.rearrange("p (t m) -> p t m", t=PACK), src.rearrange("p (m t) -> p t m", t=PACK))
+
+        def permute_on_gpsimd(e, reuse):
+            perm = sb("w1_perm%d" % e, [P, 2 * H], U8, reuse=reuse)
+            raw = w1_raw[e // 2][:, (e % 2) * 2 * H : (e % 2 + 1) * 2 * H]
+            permute_in_sweeps(perm[:].bitcast(U16), raw.bitcast(U16))
+            w1_perm[e] = perm[:]
+
         def list_columns(lo, hi):
             return slice(lo // PER_COLUMN, hi // PER_COLUMN)
 
@@ -210,24 +219,25 @@ def tile_moe_loc_mlp_silu_kernel(
 
         load_w1_words(1)
         nc.sync.dma_start(w2_all[:].bitcast(I32).rearrange("p (e c) -> p e c", e=E), w2_rows)
+        load_w1_words(2)
 
         picked_words = [sb("picked_words%d" % g, [P, S // 2], U32) for g in range(2)]
         for g in range(2):
             entries = offs2_t[:, list_columns(g * S // 2, (g + 1) * S // 2)]
             nc.vector.tensor_copy(picked_words[g][:], other_words[:].bitcast(U32).indirect(entries))
 
-        after_casts = sb("after_casts", [P, 5 * H], U8, reuse="xo_raw1")
+        after_casts = sb("after_casts", [P, 4 * H], U8, reuse="xo_raw1")
         permute_w1_words(nc.scalar.copy, 0, 2, after_casts[:, : 4 * H])
         woven = {0: weave(0, gather_own(0))}
-        w1_plane[0] = after_casts[:, 4 * H :]
-        permute_columns(nc.vector.tensor_copy, w1_plane[0], w1_stack[:], LINE)
+        w1_plane[0] = sb("w1_plane0", [P, H], U8)[:]
+        permute_in_sweeps(w1_plane[0], w1_stack[:])
+        permute_on_gpsimd(3, "w1_stack")
         permute_w1_words(nc.scalar.copy, 2, 3, placed("w1_perm2", [P, 2 * H], U8, 4 * H)[:])
         woven[1] = weave(1, gather_own(1))
         for e in range(1, 4):
             move_plane(e)
         load_plane(w2_plane[:], w2_scales.rearrange("e s b n -> (e s) b n"), N)
         load_plane(other_plane[:, :Q], x_scales, Q)
-        load_w1_words(2)
         for e in range(4, E):
             move_plane(e)
 
@@ -252,11 +262,8 @@ def tile_moe_loc_mlp_silu_kernel(
                     row_block(acc[:, b * C : (b + 1) * C], done, b, *h_codes[done])
                 for b in blocks:
                     nc.scalar.copy(y[b][:, done * C : (done + 1) * C], acc[:, b * C : (b + 1) * C])
-            if e == 1:
-                permute_w1_words(nc.vector.tensor_copy, 3, 4, sb("w1_perm3", [P, 2 * H], U8, reuse="x0_plane")[:])
-            if e == 3:
-                perm = sb("w1_perm4", [P, 2 * 2 * H], U8, reuse="x2_plane")
-                permute_w1_words(nc.vector.tensor_copy, 4, E, perm[:])
+            if e < 2:
+                permute_on_gpsimd(4 + e, "woven%d" % e)
             if e == 1:
                 nc.sync.dma_start(pos_t[0][:], pos1)
                 nc.sync.dma_start(pos_t[1][:], pos2)

@@ -32,6 +32,7 @@ WINDOW = 2 * Q
 PIECES = ((0, 0, 768), (1, 0, 384), (1, 384, 640), (1, 640, 768))
 PAIRS = E // 2
 VECTOR_CAST = 160
+VECTOR_COPIES = (0, 1)
 DEFERRED = E - 2
 
 FINISHED = {1: (0,), 2: (1,), 3: (2,), 5: (3, 4), 6: (5,)}
@@ -108,23 +109,11 @@ def tile_moe_loc_mlp_silu_kernel(
                 w1_raw[g][:].bitcast(I32).rearrange("p (e c) -> p e c", e=2), w1_rows[:, 2 * g : 2 * g + 2, :]
             )
 
-        def permute_columns(copy, dst, src, run, experts=1):
-            copy(
-                dst.rearrange("p (e t c i) -> p e c t i", e=experts, t=PACK, i=run),
-                src.rearrange("p (e c i t) -> p e c t i", e=experts, t=PACK, i=run),
-            )
-
         def move_plane(e):
             nc.sync.dma_start(
                 w1_plane[e][0:MOVED_ROWS, :].bitcast(I32),
                 w1_plane[0][PACK * e : PACK * e + MOVED_ROWS, :].bitcast(I32),
             )
-
-        def permute_w1_words(copy, lo, hi, perm):
-            raw = w1_raw[lo // 2][:, (lo % 2) * 2 * H : (lo % 2 + hi - lo) * 2 * H]
-            permute_columns(copy, perm.bitcast(U16), raw.bitcast(U16), LINE // 2, hi - lo)
-            for e in range(lo, hi):
-                w1_perm[e] = perm[:, (e - lo) * 2 * H : (e - lo + 1) * 2 * H]
 
         def permute_in_sweeps(dst, src):
             nc.gpsimd.tensor_copy(dst.rearrange("p (t m) -> p t m", t=PACK), src.rearrange("p (m t) -> p t m", t=PACK))
@@ -138,10 +127,16 @@ def tile_moe_loc_mlp_silu_kernel(
         def list_columns(lo, hi):
             return slice(lo // PER_COLUMN, hi // PER_COLUMN)
 
-        def quantize(name, values, width):
+        def quantize(name, values, width, parts=1):
             codes = sb(name + "_codes", [P, width], U32)
             plane = sb(name + "_plane", [P, width], U8)
-            nc.vector.quantize_mx(out=codes[:].bitcast(FP8X4), scales=plane[:], in_=values)
+            step = width // parts
+            for lo in range(0, width, step):
+                nc.vector.quantize_mx(
+                    out=codes[:, lo : lo + step].bitcast(FP8X4),
+                    scales=plane[:, lo : lo + step],
+                    in_=values[:, PACK * lo : PACK * (lo + step)],
+                )
             return codes[:], plane[:]
 
         def gather_own(e):
@@ -158,10 +153,12 @@ def tile_moe_loc_mlp_silu_kernel(
 
         def weave(e, halves):
             woven = sb("woven%d" % e, [P, 2 * C], U32, reuse="x%d_codes" % (e - 2) if e >= 2 else "")
-            nc.scalar.copy(
-                woven[:].rearrange("p (s u) -> p s u", u=2),
-                halves[:].rearrange("p (u s) -> p s u", u=2),
-            )
+            step = C if e else P
+            for lo in range(0, C, step):
+                nc.scalar.copy(
+                    woven[:].rearrange("p (s u) -> p s u", u=2)[:, lo : lo + step, :],
+                    halves[:].rearrange("p (u s) -> p s u", u=2)[:, lo : lo + step, :],
+                )
             return woven
 
         def first_layer(hidden, e, codes, plane, blocks=range(C // P)):
@@ -226,13 +223,11 @@ def tile_moe_loc_mlp_silu_kernel(
             entries = offs2_t[:, list_columns(g * S // 2, (g + 1) * S // 2)]
             nc.vector.tensor_copy(picked_words[g][:], other_words[:].bitcast(U32).indirect(entries))
 
-        after_casts = sb("after_casts", [P, 4 * H], U8, reuse="xo_raw1")
-        permute_w1_words(nc.scalar.copy, 0, 2, after_casts[:, : 4 * H])
         woven = {0: weave(0, gather_own(0))}
         w1_plane[0] = sb("w1_plane0", [P, H], U8)[:]
         permute_in_sweeps(w1_plane[0], w1_stack[:])
-        permute_on_gpsimd(3, "w1_stack")
-        permute_w1_words(nc.scalar.copy, 2, 3, placed("w1_perm2", [P, 2 * H], U8, 4 * H)[:])
+        permute_on_gpsimd(0, "w1_stack")
+        permute_on_gpsimd(1, "")
         woven[1] = weave(1, gather_own(1))
         for e in range(1, 4):
             move_plane(e)
@@ -245,25 +240,29 @@ def tile_moe_loc_mlp_silu_kernel(
         h_codes = {}
         for e in range(E + 1):
             if e < E:
-                x_codes, x_plane = quantize("x%d" % e, woven[e][:].bitcast(BF16), C)
+                x_codes, x_plane = quantize("x%d" % e, woven[e][:].bitcast(BF16), C, 1 if e else 2)
             if e + 2 < E:
                 halves = gather_own(e + 2)
             if e < E:
                 hidden[e] = sb("hidden%d" % e, [P, PACK * C], BF16)
                 first_layer(hidden[e][:], e, x_codes, x_plane)
+            if e - 2 in VECTOR_COPIES:
+                acc = bank("first", FIRST_BANKS)
+                row_block(acc[:, :C], e - 2, 1, *h_codes[e - 2])
+                nc.vector.tensor_copy(y[1][:, (e - 2) * C : (e - 1) * C], acc[:, :C])
             if e + 2 < E:
                 woven[e + 2] = weave(e + 2, halves)
             if e >= 1:
                 h_codes[e - 1] = quantize("h%d" % (e - 1), hidden[e - 1][:], C)
             for done in FINISHED.get(e, ()):
                 acc = bank("second", SECOND_BANKS)
-                blocks = range(1 if done >= DEFERRED else ROW_BLOCKS)
+                blocks = range(1 if done >= DEFERRED or done in VECTOR_COPIES else ROW_BLOCKS)
                 for b in blocks:
                     row_block(acc[:, b * C : (b + 1) * C], done, b, *h_codes[done])
                 for b in blocks:
                     nc.scalar.copy(y[b][:, done * C : (done + 1) * C], acc[:, b * C : (b + 1) * C])
-            if e < 2:
-                permute_on_gpsimd(4 + e, "woven%d" % e)
+            if e + 2 < E:
+                permute_on_gpsimd(e + 2, "woven%d" % e)
             if e == 1:
                 nc.sync.dma_start(pos_t[0][:], pos1)
                 nc.sync.dma_start(pos_t[1][:], pos2)

@@ -31,8 +31,9 @@ WINDOW = 2 * Q
 
 PIECES = ((0, 0, 768), (1, 0, 384), (1, 384, 640), (1, 640, 768))
 PAIRS = E // 2
-VECTOR_CAST = 160
-VECTOR_COPIES = (0, 1)
+XO_PIECES = ((0, 0, T), (1, 0, T // 2), (1, T // 2, T))
+GPSIMD_CAST = 320
+VECTOR_COPIES = (1,)
 DEFERRED = E - 2
 
 FINISHED = {1: (0,), 2: (1,), 3: (2,), 5: (3, 4), 6: (5,)}
@@ -68,7 +69,9 @@ def tile_moe_loc_mlp_silu_kernel(
         pos_t = [sb("pos1_t", [P, T // PER_COLUMN], U16), sb("pos2_t", [P, T // PER_COLUMN], U16)]
         other_words = sb("other_words", [P, WINDOW], I32)
         other_plane = sb("other_plane", [P, WINDOW], U8)
-        xo_raw = [sb("xo_raw%d" % u, [P, 2 * T], F32) for u in range(2)]
+        xo_raw = {
+            (u, lo): sb("xo_raw%d_%d" % (u, lo), [P, 2, hi - lo], F32) for u, lo, hi in XO_PIECES
+        }
         xo_pairs = [sb("xo_pairs%d" % u, [P, 2 * T], BF16) for u in range(2)]
         w1_raw = [sb("w1_raw%d" % g, [P, 2 * 2 * H], U8) for g in range(PAIRS)]
         w1_stack = sb("w1_stack", [P, H], U8)
@@ -86,7 +89,7 @@ def tile_moe_loc_mlp_silu_kernel(
         nc.vector.memset(w1_moved[:].bitcast(I32), 0)
         nc.vector.memset(other_plane[:].bitcast(I32), 0)
 
-        xo_halves = xo.rearrange("(p u j) t -> p u (j t)", u=2, j=2)
+        xo_halves = xo.rearrange("(p u j) t -> p u j t", u=2, j=2)
         w1_rows = w1_words.bitcast(I32).rearrange("e s p c -> p (e s) c")
         w2_rows = w2_words.bitcast(I32).rearrange("e s p c -> p (e s) c")
         out_rows = out.rearrange("(b p) c -> p b c", p=P)
@@ -195,8 +198,8 @@ def tile_moe_loc_mlp_silu_kernel(
 
         nc.sync.dma_start(offs2_t[:], offs2)
         nc.scalar.dma_start(other_words[:, :Q], x_words[0].rearrange("p t d -> p (t d)").bitcast(I32))
-        for u in range(2):
-            nc.scalar.dma_start(xo_raw[u][:], xo_halves[:, u, :])
+        for u, lo, hi in XO_PIECES:
+            nc.scalar.dma_start(xo_raw[u, lo][:], xo_halves[:, u, :, lo:hi])
         warm = sb("warm", [P, 2], F32)
         nc.gpsimd.memset(warm[:, 0:1], 0.0)
         nc.scalar.activation(warm[:, 1:2], warm[:, 0:1], SILU)
@@ -204,15 +207,15 @@ def tile_moe_loc_mlp_silu_kernel(
         load_w1_stack()
         load_w1_words(0)
 
-        def cast(copy, u, lo, hi):
+        def cast(copy, u, first, lo, hi):
             copy(
                 xo_pairs[u][:].rearrange("p (t j) -> p t j", j=2)[:, lo:hi, :],
-                xo_raw[u][:].rearrange("p (j t) -> p t j", j=2)[:, lo:hi, :],
+                xo_raw[u, first][:].rearrange("p j t -> p t j")[:, lo - first : hi - first, :],
             )
 
-        cast(nc.scalar.copy, 0, 0, T)
-        cast(nc.vector.tensor_copy, 1, 0, VECTOR_CAST)
-        cast(nc.scalar.copy, 1, VECTOR_CAST, T)
+        cast(nc.gpsimd.tensor_copy, 0, 0, T - GPSIMD_CAST, T)
+        for u, lo, hi in XO_PIECES:
+            cast(nc.scalar.copy, u, lo, lo, hi if u else hi - GPSIMD_CAST)
 
         load_w1_words(1)
         nc.sync.dma_start(w2_all[:].bitcast(I32).rearrange("p (e c) -> p e c", e=E), w2_rows)
@@ -223,11 +226,15 @@ def tile_moe_loc_mlp_silu_kernel(
             entries = offs2_t[:, list_columns(g * S // 2, (g + 1) * S // 2)]
             nc.vector.tensor_copy(picked_words[g][:], other_words[:].bitcast(U32).indirect(entries))
 
+        w1_perm[1] = sb("w1_perm1", [P, 2 * H], U8, reuse="xo_raw1_%d" % (T // 2))[:]
+        nc.scalar.copy(
+            w1_perm[1].bitcast(U16).rearrange("p (t c i) -> p c t i", t=PACK, i=LINE // 2),
+            w1_raw[0][:, 2 * H :].bitcast(U16).rearrange("p (c i t) -> p c t i", t=PACK, i=LINE // 2),
+        )
         woven = {0: weave(0, gather_own(0))}
         w1_plane[0] = sb("w1_plane0", [P, H], U8)[:]
         permute_in_sweeps(w1_plane[0], w1_stack[:])
         permute_on_gpsimd(0, "w1_stack")
-        permute_on_gpsimd(1, "")
         woven[1] = weave(1, gather_own(1))
         for e in range(1, 4):
             move_plane(e)

@@ -33,7 +33,8 @@ PIECES = ((0, 0, 768), (1, 0, 384), (1, 384, 640), (1, 640, 768))
 PAIRS = E // 2
 XO_PIECES = ((0, 0, T), (1, 0, T // 2), (1, T // 2, T))
 GPSIMD_CAST = 320
-VECTOR_COPIES = (1,)
+SHARED_WEAVES = (4, 5)
+VECTOR_COPIES = ()
 DEFERRED = E - 2
 
 FINISHED = {1: (0,), 2: (1,), 3: (2,), 5: (3, 4), 6: (5,)}
@@ -130,16 +131,13 @@ def tile_moe_loc_mlp_silu_kernel(
         def list_columns(lo, hi):
             return slice(lo // PER_COLUMN, hi // PER_COLUMN)
 
-        def quantize(name, values, width, parts=1):
+        def quantize(name, parts, width):
             codes = sb(name + "_codes", [P, width], U32)
             plane = sb(name + "_plane", [P, width], U8)
-            step = width // parts
-            for lo in range(0, width, step):
-                nc.vector.quantize_mx(
-                    out=codes[:, lo : lo + step].bitcast(FP8X4),
-                    scales=plane[:, lo : lo + step],
-                    in_=values[:, PACK * lo : PACK * (lo + step)],
-                )
+            step = width // len(parts)
+            for k, values in enumerate(parts):
+                cols = slice(k * step, (k + 1) * step)
+                nc.vector.quantize_mx(out=codes[:, cols].bitcast(FP8X4), scales=plane[:, cols], in_=values)
             return codes[:], plane[:]
 
         def gather_own(e):
@@ -155,14 +153,26 @@ def tile_moe_loc_mlp_silu_kernel(
             return halves
 
         def weave(e, halves):
-            woven = sb("woven%d" % e, [P, 2 * C], U32, reuse="x%d_codes" % (e - 2) if e >= 2 else "")
+            pairs = halves[:].rearrange("p (u s) -> p s u", u=2)
+            reuse = "x%d_codes" % (e - 2) if e >= 2 else ""
+            if e in SHARED_WEAVES:
+                low = sb("woven%d" % e, [P, 2 * P], U32, reuse=reuse)
+                nc.scalar.copy(low[:].rearrange("p (s u) -> p s u", u=2), pairs[:, :P, :])
+                return [low[:].bitcast(BF16)]
+            woven = sb("woven%d" % e, [P, 2 * C], U32, reuse=reuse)
             step = C if e else P
             for lo in range(0, C, step):
                 nc.scalar.copy(
-                    woven[:].rearrange("p (s u) -> p s u", u=2)[:, lo : lo + step, :],
-                    halves[:].rearrange("p (u s) -> p s u", u=2)[:, lo : lo + step, :],
+                    woven[:].rearrange("p (s u) -> p s u", u=2)[:, lo : lo + step, :], pairs[:, lo : lo + step, :]
                 )
-            return woven
+            return [woven[:, 2 * lo : 2 * (lo + step)].bitcast(BF16) for lo in range(0, C, step)]
+
+        def weave_rest(e, halves):
+            high = sb("high%d" % e, [P, 2 * P], U32, reuse="woven%d" % (e - 1))
+            nc.gpsimd.tensor_copy(
+                high[:].rearrange("p (s u) -> p s u", u=2), halves[:].rearrange("p (u s) -> p s u", u=2)[:, P:, :]
+            )
+            return high[:].bitcast(BF16)
 
         def first_layer(hidden, e, codes, plane, blocks=range(C // P)):
             for block in blocks:
@@ -226,16 +236,21 @@ def tile_moe_loc_mlp_silu_kernel(
             entries = offs2_t[:, list_columns(g * S // 2, (g + 1) * S // 2)]
             nc.vector.tensor_copy(picked_words[g][:], other_words[:].bitcast(U32).indirect(entries))
 
-        w1_perm[1] = sb("w1_perm1", [P, 2 * H], U8, reuse="xo_raw1_%d" % (T // 2))[:]
-        nc.scalar.copy(
-            w1_perm[1].bitcast(U16).rearrange("p (t c i) -> p c t i", t=PACK, i=LINE // 2),
-            w1_raw[0][:, 2 * H :].bitcast(U16).rearrange("p (c i t) -> p c t i", t=PACK, i=LINE // 2),
-        )
+        def permute_on_scalar(e, perm):
+            raw = w1_raw[e // 2][:, (e % 2) * 2 * H : (e % 2 + 1) * 2 * H]
+            nc.scalar.copy(
+                perm.bitcast(U16).rearrange("p (t c i) -> p c t i", t=PACK, i=LINE // 2),
+                raw.bitcast(U16).rearrange("p (c i t) -> p c t i", t=PACK, i=LINE // 2),
+            )
+            w1_perm[e] = perm
+
+        permute_on_scalar(1, sb("w1_perm1", [P, 2 * H], U8, reuse="xo_raw1_%d" % (T // 2))[:])
         woven = {0: weave(0, gather_own(0))}
         w1_plane[0] = sb("w1_plane0", [P, H], U8)[:]
         permute_in_sweeps(w1_plane[0], w1_stack[:])
         permute_on_gpsimd(0, "w1_stack")
         woven[1] = weave(1, gather_own(1))
+        permute_on_scalar(2, placed("w1_perm2", [P, 2 * H], U8, 4 * H)[:])
         for e in range(1, 4):
             move_plane(e)
         load_plane(w2_plane[:], w2_scales.rearrange("e s b n -> (e s) b n"), N)
@@ -247,7 +262,9 @@ def tile_moe_loc_mlp_silu_kernel(
         h_codes = {}
         for e in range(E + 1):
             if e < E:
-                x_codes, x_plane = quantize("x%d" % e, woven[e][:].bitcast(BF16), C, 1 if e else 2)
+                x_codes, x_plane = quantize("x%d" % e, woven[e], C)
+            if e + 1 in SHARED_WEAVES:
+                woven[e + 1].append(weave_rest(e + 1, halves))
             if e + 2 < E:
                 halves = gather_own(e + 2)
             if e < E:
@@ -260,7 +277,7 @@ def tile_moe_loc_mlp_silu_kernel(
             if e + 2 < E:
                 woven[e + 2] = weave(e + 2, halves)
             if e >= 1:
-                h_codes[e - 1] = quantize("h%d" % (e - 1), hidden[e - 1][:], C)
+                h_codes[e - 1] = quantize("h%d" % (e - 1), [hidden[e - 1][:]], C)
             for done in FINISHED.get(e, ()):
                 acc = bank("second", SECOND_BANKS)
                 blocks = range(1 if done >= DEFERRED or done in VECTOR_COPIES else ROW_BLOCKS)
@@ -268,8 +285,8 @@ def tile_moe_loc_mlp_silu_kernel(
                     row_block(acc[:, b * C : (b + 1) * C], done, b, *h_codes[done])
                 for b in blocks:
                     nc.scalar.copy(y[b][:, done * C : (done + 1) * C], acc[:, b * C : (b + 1) * C])
-            if e + 2 < E:
-                permute_on_gpsimd(e + 2, "woven%d" % e)
+            if e + 3 < E:
+                permute_on_gpsimd(e + 3, "woven%d" % e)
             if e == 1:
                 nc.sync.dma_start(pos_t[0][:], pos1)
                 nc.sync.dma_start(pos_t[1][:], pos2)
@@ -279,14 +296,14 @@ def tile_moe_loc_mlp_silu_kernel(
         picked_plane = {}
         last = E - 1
         for lo, hi, reuse in (
-            (0, 1, "halves%d" % (last - 1)),
-            (1, 4, "halves%d" % last),
+            (0, 2, "halves%d" % (last - 1)),
+            (2, 4, "halves%d" % last),
             (4, E, "hidden%d" % last),
         ):
             if lo:
                 part = sb("picked_plane%d" % lo, [P, (hi - lo) * C], U8, reuse=reuse)
             else:
-                part = placed("picked_plane0", [P, C], U8, 0)
+                part = placed("picked_plane0", [P, 2 * C], U8, 0)
             nc.vector.tensor_copy(part[:], other_plane[:].indirect(offs2_t[:, list_columns(lo * C, hi * C)]))
             for e in range(lo, hi):
                 picked_plane[e] = part[:, (e - lo) * C : (e - lo + 1) * C]
@@ -311,7 +328,7 @@ def tile_moe_loc_mlp_silu_kernel(
 
         def quantize_group(g):
             lo, hi = groups[g]
-            group_codes[g] = quantize("group%d" % g, group_hidden[g][:], (hi - lo) * C)
+            group_codes[g] = quantize("group%d" % g, [group_hidden[g][:]], (hi - lo) * C)
 
         def pair_rows(g, b):
             codes, plane = group_codes[g]
@@ -367,7 +384,7 @@ def tile_moe_loc_mlp_silu_kernel(
         product(0, 0)
         product(0, 1)
         quantize_group(0)
-        stage("stage1", [(0, 2), (1, 0)], reuse="picked_plane1")
+        stage("stage1", [(0, 2), (1, 0)], reuse="picked_plane2")
         product(1, 0)
         add_and_store(0)
         pair_rows(0, 0)

@@ -35,7 +35,7 @@ XO_PIECES = ((0, 0, T), (1, 0, T // 2), (1, T // 2, T))
 GPSIMD_CAST = 320
 SHARED_WEAVES = (4, 5)
 VECTOR_COPIES = ()
-DEFERRED = E - 2
+DEFERRED = E - 1
 
 FINISHED = {1: (0,), 2: (1,), 3: (2,), 5: (3, 4), 6: (5,)}
 
@@ -298,7 +298,8 @@ def tile_moe_loc_mlp_silu_kernel(
         for lo, hi, reuse in (
             (0, 2, "halves%d" % (last - 1)),
             (2, 4, "halves%d" % last),
-            (4, E, "hidden%d" % last),
+            (4, 5, "hidden%d" % (last - 1)),
+            (5, E, "hidden%d" % last),
         ):
             if lo:
                 part = sb("picked_plane%d" % lo, [P, (hi - lo) * C], U8, reuse=reuse)
@@ -311,7 +312,7 @@ def tile_moe_loc_mlp_silu_kernel(
         acc = bank("second", SECOND_BANKS)
         for e in range(DEFERRED, E):
             row_block(acc[:, (e - DEFERRED) * C : (e - DEFERRED + 1) * C], e, 1, *h_codes[e])
-        nc.scalar.copy(y[1][:, DEFERRED * C :], acc[:])
+        nc.scalar.copy(y[1][:, DEFERRED * C :], acc[:, : (E - DEFERRED) * C])
 
         groups = ((0, 2), (2, 4), (4, 5), (5, 6))
         group_hidden = [sb("other_hidden%d" % lo, [P, (hi - lo) * PACK * C], BF16) for lo, hi in groups]
@@ -397,7 +398,7 @@ def tile_moe_loc_mlp_silu_kernel(
         pair_rows(1, 0)
         other_block(5, 1)
         quantize_group(2)
-        stage("stage2b", [(1, 2), (3, 0)], reuse="picked_plane4")
+        stage("stage2b", [(1, 2), (3, 0)], reuse="picked_plane5")
         add_and_store(1)
         product(3, 0)
         quantize_group(3)

@@ -15,6 +15,7 @@ U8 = mybir.dt.uint8
 FP8X4 = mybir.dt.float8_e4m3fn_x4
 FP4X4 = mybir.dt.float4_e2m1fn_x4
 SILU = mybir.ActivationFunctionType.Silu
+COPY = mybir.ActivationFunctionType.Copy
 MULT = mybir.AluOpType.mult
 ADD = mybir.AluOpType.add
 
@@ -279,7 +280,7 @@ def tile_moe_loc_mlp_silu_kernel(
             if e >= 1:
                 h_codes[e - 1] = quantize("h%d" % (e - 1), [hidden[e - 1][:]], C)
             for done in FINISHED.get(e, ()):
-                acc = bank("second", SECOND_BANKS)
+                acc = bank("first", FIRST_BANKS, 1) if done == E - 3 else bank("second", SECOND_BANKS)
                 blocks = range(1 if done >= DEFERRED or done in VECTOR_COPIES else ROW_BLOCKS)
                 for b in blocks:
                     row_block(acc[:, b * C : (b + 1) * C], done, b, *h_codes[done])
@@ -298,7 +299,7 @@ def tile_moe_loc_mlp_silu_kernel(
         for lo, hi, reuse in (
             (0, 2, "halves%d" % (last - 1)),
             (2, 4, "halves%d" % last),
-            (4, 5, "hidden%d" % (last - 1)),
+            (4, 5, "h%d_codes" % (last - 2)),
             (5, E, "hidden%d" % last),
         ):
             if lo:
@@ -341,16 +342,20 @@ def tile_moe_loc_mlp_silu_kernel(
             nc.scalar.copy(z[:], acc[:])
             nc.sync.dma_start(out_rows[:, b, T + 2 * g * C : T + 2 * (g + 1) * C], z[:])
 
-        def single_rows(g, skip=0):
+        def single_rows(g, skip=0, parts=1):
             e = groups[g][0]
             acc = bank("first", FIRST_BANKS, skip)
             for b in range(ROW_BLOCKS):
                 row_block(acc[:, b * C : (b + 1) * C], e, b, *group_codes[g])
             z = sb("z%d" % e, [P, ROW_BLOCKS * C], F32)
-            nc.scalar.copy(z[:], acc[:])
-            nc.sync.dma_start(
-                out_rows[:, :, T + e * C : T + (e + 1) * C], z[:].rearrange("p (b c) -> p b c", b=ROW_BLOCKS)
-            )
+            step = ROW_BLOCKS // parts
+            for b in range(0, ROW_BLOCKS, step):
+                cols = slice(b * C, (b + step) * C)
+                nc.scalar.copy(z[:, cols], acc[:, cols])
+                nc.sync.dma_start(
+                    out_rows[:, b : b + step, T + e * C : T + (e + 1) * C],
+                    z[:, cols].rearrange("p (b c) -> p b c", b=step),
+                )
 
         for e in range(4):
             for block in range(C // P):
@@ -403,11 +408,14 @@ def tile_moe_loc_mlp_silu_kernel(
         product(3, 0)
         quantize_group(3)
         pair_rows(1, 1)
+        b, lo, hi = PIECES[2]
+        fetched = sb("fetched", [P, hi - lo], F32)
+        nc.scalar.activation(fetched[:], y[b][:].indirect(pos_t[0][:, list_columns(lo, hi)]), COPY)
         single_rows(2, skip=FIRST_BANKS - 2)
-        single_rows(3)
+        single_rows(3, parts=ROW_BLOCKS)
         stage("stage3", [(2, 0), (2, 1), (2, 2), (3, 1), (3, 2)], reuse="group2_codes")
-        product(2, 0)
         product(2, 1)
+        nc.vector.tensor_tensor(room[2, 0], fetched[:], gate_t[0][:, lo:hi], MULT)
         product(3, 1)
         add_and_store(2)
         add_and_store(3)

from contextlib import ExitStack

import concourse.mybir as mybir

K, T, Q, E, C, H, N = 512, 768, 512, 6, 256, 512, 256
S = E * C
FLOPS = 2 * 2 * S * (K * H + H * N)

F32 = mybir.dt.float32
BF16 = mybir.dt.bfloat16
I32 = mybir.dt.int32
U32 = mybir.dt.uint32
U16 = mybir.dt.uint16
U8 = mybir.dt.uint8
FP8X4 = mybir.dt.float8_e4m3fn_x4
FP4X4 = mybir.dt.float4_e2m1fn_x4
SILU = mybir.ActivationFunctionType.Silu
COPY = mybir.ActivationFunctionType.Copy
MULT = mybir.AluOpType.mult
ADD = mybir.AluOpType.add

P = 128
PACK = 4
QUADRANT = 32
SCALE_ROWS = 16
PER_COLUMN = 16
LINE = 16
ROW_BLOCKS = N // P
FIRST_BANKS, SECOND_BANKS = 4, 3
MOVED_ROWS = 3 * QUADRANT + PACK
WINDOW = 2 * Q

PIECES = ((0, 0, 768), (1, 0, 384), (1, 384, 640), (1, 640, 768))
PAIRS = E // 2
XO_PIECES = ((0, 0, T), (1, 0, T // 2), (1, T // 2, T))
GPSIMD_CAST = 320
SHARED_WEAVES = (4, 5)
VECTOR_COPIES = ()
DEFERRED = E - 1

FINISHED = {1: (0,), 2: (1,), 3: (2,), 5: (3, 4), 6: (5,)}


def tile_moe_loc_mlp_silu_kernel(
    tc, x_words, x_scales, xo, w1_words, w1_scales, w2_words, w2_scales, gate, offs, pos1, pos2, offs2, out
):
    nc = tc.nc
    with ExitStack() as ctx:
        keep = ctx.enter_context(tc.tile_pool(name="keep", bufs=1))
        shared = ctx.enter_context(tc.tile_pool(name="shared", bufs=1))
        psum = ctx.enter_context(tc.psum_pool(name="psum", bufs=1))

        turns = {"first": 0, "second": 0}

        def bank(layer, count, skip=0):
            tag = "%s%d" % (layer, (turns[layer] + skip) % count)
            turns[layer] = turns[layer] + skip + 1
            return psum.tile([P, PACK * P], F32, name=tag, tag=tag)

        space = {}

        def sb(name, shape, dtype, reuse=""):
            space[name] = space[reuse] if reuse else name
            return keep.tile(shape, dtype, name=name, tag=space[name], align_bytes=64)

        def placed(name, shape, dtype, offset):
            return shared.tile(shape, dtype, name=name, tag=name, offset=offset, align_bytes=64)

        offs_t = sb("offs_t", [P, S // PER_COLUMN], U16)
        offs2_t = sb("offs2_t", [P, S // PER_COLUMN], U16)
        pos_t = [sb("pos1_t", [P, T // PER_COLUMN], U16), sb("pos2_t", [P, T // PER_COLUMN], U16)]
        other_words = sb("other_words", [P, WINDOW], I32)
        other_plane = sb("other_plane", [P, WINDOW], U8)
        xo_raw = {
            (u, lo): sb("xo_raw%d_%d" % (u, lo), [P, 2, hi - lo], F32) for u, lo, hi in XO_PIECES
        }
        xo_pairs = [sb("xo_pairs%d" % u, [P, 2 * T], BF16) for u in range(2)]
        w1_raw = [sb("w1_raw%d" % g, [P, 2 * 2 * H], U8) for g in range(PAIRS)]
        w1_stack = sb("w1_stack", [P, H], U8)
        w1_perm = {}
        w1_moved = sb("w1_moved", [P, (E - 1) * H], U8)
        w1_plane = {e: w1_moved[:, (e - 1) * H : e * H] for e in range(1, E)}
        w2_all = sb("w2_all", [P, E * 2 * N], U8)
        w2_plane = sb("w2_plane", [P, E * N], U8)
        gate_t = [sb("gate%d" % r, [P, T], F32) for r in range(2)]
        y = [sb("y%d" % b, [P, S], F32) for b in range(ROW_BLOCKS)]

        nc.vector.memset(w1_stack[:].bitcast(I32), 0)
        nc.vector.memset(other_words[:, Q:], 0)
        nc.vector.memset(w2_plane[:].bitcast(I32), 0)
        nc.vector.memset(w1_moved[:].bitcast(I32), 0)
        nc.vector.memset(other_plane[:].bitcast(I32), 0)

        xo_halves = xo.rearrange("(p u j) t -> p u j t", u=2, j=2)
        w1_rows = w1_words.bitcast(I32).rearrange("e s p c -> p (e s) c")
        w2_rows = w2_words.bitcast(I32).rearrange("e s p c -> p (e s) c")
        out_rows = out.rearrange("(b p) c -> p b c", p=P)

        def load_plane(plane, scales, width):
            dst = plane.bitcast(I32).rearrange("p (m c) -> p m c", c=width // 4)
            rows = scales.bitcast(I32)
            for r in range(PACK):
                nc.sync.dma_start(dst[r:P:QUADRANT], rows[:, r:SCALE_ROWS:PACK, :].rearrange("m q c -> q m c"))

        def load_w1_stack():
            for q in range(P // QUADRANT):
                nc.sync.dma_start(
                    w1_stack[QUADRANT * q : QUADRANT * q + PACK * E, :].bitcast(I32),
                    w1_scales.bitcast(I32)[:, 0, PACK * q : PACK * (q + 1), :],
                )

        def load_w1_words(g):
            nc.sync.dma_start(
                w1_raw[g][:].bitcast(I32).rearrange("p (e c) -> p e c", e=2), w1_rows[:, 2 * g : 2 * g + 2, :]
            )

        def move_plane(e):
            nc.sync.dma_start(
                w1_plane[e][0:MOVED_ROWS, :].bitcast(I32),
                w1_plane[0][PACK * e : PACK * e + MOVED_ROWS, :].bitcast(I32),
            )

        def permute_in_sweeps(dst, src):
            nc.gpsimd.tensor_copy(dst.rearrange("p (t m) -> p t m", t=PACK), src.rearrange("p (m t) -> p t m", t=PACK))

        def permute_on_gpsimd(e, reuse):
            perm = sb("w1_perm%d" % e, [P, 2 * H], U8, reuse=reuse)
            raw = w1_raw[e // 2][:, (e % 2) * 2 * H : (e % 2 + 1) * 2 * H]
            permute_in_sweeps(perm[:].bitcast(U16), raw.bitcast(U16))
            w1_perm[e] = perm[:]

        def list_columns(lo, hi):
            return slice(lo // PER_COLUMN, hi // PER_COLUMN)

        def quantize(name, parts, width):
            codes = sb(name + "_codes", [P, width], U32)
            plane = sb(name + "_plane", [P, width], U8)
            step = width // len(parts)
            for k, values in enumerate(parts):
                cols = slice(k * step, (k + 1) * step)
                nc.vector.quantize_mx(out=codes[:, cols].bitcast(FP8X4), scales=plane[:, cols], in_=values)
            return codes[:], plane[:]

        def gather_own(e):
            if e % 2:
                halves = sb("halves%d" % e, [P, 2 * C], U32, reuse="halves%d" % (e - 2) if e >= 2 else "")
            else:
                halves = placed("halves%d" % e, [P, 2 * C], U32, 0 if e else 2 * H)
            for u in range(2):
                nc.vector.tensor_copy(
                    halves[:, u * C : (u + 1) * C],
                    xo_pairs[u][:].bitcast(U32).indirect(offs_t[:, list_columns(e * C, (e + 1) * C)]),
                )
            return halves

        def weave(e, halves):
            pairs = halves[:].rearrange("p (u s) -> p s u", u=2)
            reuse = "x%d_codes" % (e - 2) if e >= 2 else ""
            if e in SHARED_WEAVES:
                low = sb("woven%d" % e, [P, 2 * P], U32, reuse=reuse)
                nc.scalar.copy(low[:].rearrange("p (s u) -> p s u", u=2), pairs[:, :P, :])
                return [low[:].bitcast(BF16)]
            woven = sb("woven%d" % e, [P, 2 * C], U32, reuse=reuse)
            step = C if e else P
            for lo in range(0, C, step):
                nc.scalar.copy(
                    woven[:].rearrange("p (s u) -> p s u", u=2)[:, lo : lo + step, :], pairs[:, lo : lo + step, :]
                )
            return [woven[:, 2 * lo : 2 * (lo + step)].bitcast(BF16) for lo in range(0, C, step)]

        def weave_rest(e, halves):
            high = sb("high%d" % e, [P, 2 * P], U32, reuse="woven%d" % (e - 1))
            nc.gpsimd.tensor_copy(
                high[:].rearrange("p (s u) -> p s u", u=2), halves[:].rearrange("p (u s) -> p s u", u=2)[:, P:, :]
            )
            return high[:].bitcast(BF16)

        def first_layer(hidden, e, codes, plane, blocks=range(C // P)):
            for block in blocks:
                cols = slice(block * P, (block + 1) * P)
                acc = bank("first", FIRST_BANKS)
                for t in range(PACK):
                    nc.tensor.matmul_mx(
                        out=acc[:, t * P : (t + 1) * P],
                        lhsT=w1_perm[e][:, t * 2 * P : (t + 1) * 2 * P].bitcast(FP4X4),
                        lhsT_scale=w1_plane[e][:, t * P : (t + 1) * P],
                        rhs=codes[:, cols].bitcast(FP8X4),
                        rhs_scale=plane[:, cols],
                        start=True,
                        stop=True,
                    )
                nc.scalar.activation(
                    hidden[:, block * PACK * P : (block + 1) * PACK * P].rearrange("p (s t) -> p s t", t=PACK),
                    acc[:].rearrange("p (t s) -> p s t", t=PACK),
                    SILU,
                )

        def row_block(acc, e, b, codes, plane):
            col = e * N + b * P
            nc.tensor.matmul_mx(
                out=acc,
                lhsT=w2_all[:, 2 * col : 2 * (col + P)].bitcast(FP4X4),
                lhsT_scale=w2_plane[:, col : col + P],
                rhs=codes.bitcast(FP8X4),
                rhs_scale=plane,
                start=True,
                stop=True,
            )

        nc.sync.dma_start(offs2_t[:], offs2)
        nc.scalar.dma_start(other_words[:, :Q], x_words[0].rearrange("p t d -> p (t d)").bitcast(I32))
        for u, lo, hi in XO_PIECES:
            nc.scalar.dma_start(xo_raw[u, lo][:], xo_halves[:, u, :, lo:hi])
        warm = sb("warm", [P, 2], F32)
        nc.gpsimd.memset(warm[:, 0:1], 0.0)
        nc.scalar.activation(warm[:, 1:2], warm[:, 0:1], SILU)
        nc.sync.dma_start(offs_t[:], offs)
        load_w1_stack()
        load_w1_words(0)

        def cast(copy, u, first, lo, hi):
            copy(
                xo_pairs[u][:].rearrange("p (t j) -> p t j", j=2)[:, lo:hi, :],
                xo_raw[u, first][:].rearrange("p j t -> p t j")[:, lo - first : hi - first, :],
            )

        cast(nc.gpsimd.tensor_copy, 0, 0, T - GPSIMD_CAST, T)
        for u, lo, hi in XO_PIECES:
            cast(nc.scalar.copy, u, lo, lo, hi if u else hi - GPSIMD_CAST)

        load_w1_words(1)
        nc.sync.dma_start(w2_all[:].bitcast(I32).rearrange("p (e c) -> p e c", e=E), w2_rows)
        load_w1_words(2)

        picked_words = [sb("picked_words%d" % g, [P, S // 2], U32) for g in range(2)]
        for g in range(2):
            entries = offs2_t[:, list_columns(g * S // 2, (g + 1) * S // 2)]
            nc.vector.tensor_copy(picked_words[g][:], other_words[:].bitcast(U32).indirect(entries))

        def permute_on_scalar(e, perm):
            raw = w1_raw[e // 2][:, (e % 2) * 2 * H : (e % 2 + 1) * 2 * H]
            nc.scalar.copy(
                perm.bitcast(U16).rearrange("p (t c i) -> p c t i", t=PACK, i=LINE // 2),
                raw.bitcast(U16).rearrange("p (c i t) -> p c t i", t=PACK, i=LINE // 2),
            )
            w1_perm[e] = perm

        permute_on_scalar(1, sb("w1_perm1", [P, 2 * H], U8, reuse="xo_raw1_%d" % (T // 2))[:])
        woven = {0: weave(0, gather_own(0))}
        w1_plane[0] = sb("w1_plane0", [P, H], U8)[:]
        permute_in_sweeps(w1_plane[0], w1_stack[:])
        permute_on_gpsimd(0, "w1_stack")
        woven[1] = weave(1, gather_own(1))
        permute_on_scalar(2, placed("w1_perm2", [P, 2 * H], U8, 4 * H)[:])
        for e in range(1, 4):
            move_plane(e)
        load_plane(w2_plane[:], w2_scales.rearrange("e s b n -> (e s) b n"), N)
        load_plane(other_plane[:, :Q], x_scales, Q)
        for e in range(4, E):
            move_plane(e)

        hidden = {}
        h_codes = {}
        for e in range(E + 1):
            if e < E:
                x_codes, x_plane = quantize("x%d" % e, woven[e], C)
            if e + 1 in SHARED_WEAVES:
                woven[e + 1].append(weave_rest(e + 1, halves))
            if e + 2 < E:
                halves = gather_own(e + 2)
            if e < E:
                hidden[e] = sb("hidden%d" % e, [P, PACK * C], BF16)
                first_layer(hidden[e][:], e, x_codes, x_plane)
            if e - 2 in VECTOR_COPIES:
                acc = bank("first", FIRST_BANKS)
                row_block(acc[:, :C], e - 2, 1, *h_codes[e - 2])
                nc.vector.tensor_copy(y[1][:, (e - 2) * C : (e - 1) * C], acc[:, :C])
            if e + 2 < E:
                woven[e + 2] = weave(e + 2, halves)
            if e >= 1:
                h_codes[e - 1] = quantize("h%d" % (e - 1), [hidden[e - 1][:]], C)
            for done in FINISHED.get(e, ()):
                acc = bank("first", FIRST_BANKS, 1) if done == E - 3 else bank("second", SECOND_BANKS)
                blocks = range(1 if done >= DEFERRED or done in VECTOR_COPIES else ROW_BLOCKS)
                for b in blocks:
                    row_block(acc[:, b * C : (b + 1) * C], done, b, *h_codes[done])
                for b in blocks:
                    nc.scalar.copy(y[b][:, done * C : (done + 1) * C], acc[:, b * C : (b + 1) * C])
            if e + 3 < E:
                permute_on_gpsimd(e + 3, "woven%d" % e)
            if e == 1:
                nc.sync.dma_start(pos_t[0][:], pos1)
                nc.sync.dma_start(pos_t[1][:], pos2)
                for r in range(2):
                    nc.sync.dma_start(gate_t[r][:], gate[r])

        picked_plane = {}
        last = E - 1
        for lo, hi, reuse in (
            (0, 2, "halves%d" % (last - 1)),
            (2, 4, "halves%d" % last),
            (4, 5, "h%d_codes" % (last - 2)),
            (5, E, "hidden%d" % last),
        ):
            if lo:
                part = sb("picked_plane%d" % lo, [P, (hi - lo) * C], U8, reuse=reuse)
            else:
                part = placed("picked_plane0", [P, 2 * C], U8, 0)
            nc.vector.tensor_copy(part[:], other_plane[:].indirect(offs2_t[:, list_columns(lo * C, hi * C)]))
            for e in range(lo, hi):
                picked_plane[e] = part[:, (e - lo) * C : (e - lo + 1) * C]

        acc = bank("second", SECOND_BANKS)
        for e in range(DEFERRED, E):
            row_block(acc[:, (e - DEFERRED) * C : (e - DEFERRED + 1) * C], e, 1, *h_codes[e])
        nc.scalar.copy(y[1][:, DEFERRED * C :], acc[:, : (E - DEFERRED) * C])

        groups = ((0, 2), (2, 4), (4, 5), (5, 6))
        group_hidden = [sb("other_hidden%d" % lo, [P, (hi - lo) * PACK * C], BF16) for lo, hi in groups]
        other_hidden = {}
        for g, (lo, hi) in enumerate(groups):
            for e in range(lo, hi):
                other_hidden[e] = group_hidden[g][:, (e - lo) * PACK * C : (e - lo + 1) * PACK * C]

        def other_block(e, block):
            half, k = divmod(e, E // 2)
            first_layer(other_hidden[e], e, picked_words[half][:, k * C : (k + 1) * C], picked_plane[e], [block])

        group_codes = {}

        def quantize_group(g):
            lo, hi = groups[g]
            group_codes[g] = quantize("group%d" % g, [group_hidden[g][:]], (hi - lo) * C)

        def pair_rows(g, b):
            codes, plane = group_codes[g]
            acc = bank("first", FIRST_BANKS)
            for k in range(2):
                cols = slice(k * C, (k + 1) * C)
                row_block(acc[:, cols], 2 * g + k, b, codes[:, cols], plane[:, cols])
            z = sb("z%d%d" % (g, b), [P, 2 * C], F32)
            nc.scalar.copy(z[:], acc[:])
            nc.sync.dma_start(out_rows[:, b, T + 2 * g * C : T + 2 * (g + 1) * C], z[:])

        def single_rows(g, skip=0, parts=1):
            e = groups[g][0]
            acc = bank("first", FIRST_BANKS, skip)
            for b in range(ROW_BLOCKS):
                row_block(acc[:, b * C : (b + 1) * C], e, b, *group_codes[g])
            z = sb("z%d" % e, [P, ROW_BLOCKS * C], F32)
            step = ROW_BLOCKS // parts
            for b in range(0, ROW_BLOCKS, step):
                cols = slice(b * C, (b + step) * C)
                nc.scalar.copy(z[:, cols], acc[:, cols])
                nc.sync.dma_start(
                    out_rows[:, b : b + step, T + e * C : T + (e + 1) * C],
                    z[:, cols].rearrange("p (b c) -> p b c", b=step),
                )

        for e in range(4):
            for block in range(C // P):
                other_block(e, block)
        other_block(4, 0)

        widths = [hi - lo for b, lo, hi in PIECES]
        room = {}

        def stage(name, parts, reuse=""):
            whole = sb(name, [P, sum(widths[i] for i, k in parts)], F32, reuse=reuse)
            at = 0
            for i, k in parts:
                room[i, k] = whole[:, at : at + widths[i]]
                at = at + widths[i]

        def product(i, r):
            b, lo, hi = PIECES[i]
            nc.vector.tensor_tensor(
                room[i, r],
                y[b][:].indirect(pos_t[r][:, list_columns(lo, hi)]),
                gate_t[r][:, lo:hi],
                MULT,
            )

        def add_and_store(i):
            b, lo, hi = PIECES[i]
            nc.vector.tensor_tensor(room[i, 2], room[i, 0], room[i, 1], ADD)
            nc.sync.dma_start(out_rows[:, b, lo:hi], room[i, 2])

        stage("stage0", [(0, 0), (0, 1)])
        product(0, 0)
        product(0, 1)
        quantize_group(0)
        stage("stage1", [(0, 2), (1, 0)], reuse="picked_plane2")
        product(1, 0)
        add_and_store(0)
        pair_rows(0, 0)
        other_block(4, 1)
        pair_rows(0, 1)
        other_block(5, 0)
        quantize_group(1)
        stage("stage2", [(1, 1)], reuse="group0_codes")
        product(1, 1)
        pair_rows(1, 0)
        other_block(5, 1)
        quantize_group(2)
        stage("stage2b", [(1, 2), (3, 0)], reuse="picked_plane5")
        add_and_store(1)
        product(3, 0)
        quantize_group(3)
        pair_rows(1, 1)
        b, lo, hi = PIECES[2]
        fetched = sb("fetched", [P, hi - lo], F32)
        nc.scalar.activation(fetched[:], y[b][:].indirect(pos_t[0][:, list_columns(lo, hi)]), COPY)
        single_rows(2, skip=FIRST_BANKS - 2)
        single_rows(3, parts=ROW_BLOCKS)
        stage("stage3", [(2, 0), (2, 1), (2, 2), (3, 1), (3, 2)], reuse="group2_codes")
        product(2, 1)
        nc.vector.tensor_tensor(room[2, 0], fetched[:], gate_t[0][:, lo:hi], MULT)
        product(3, 1)
        add_and_store(2)
        add_and_store(3)
